import numpy as np
import ml_dtypes


def mxq(x, axis, fmt="e4m3"):
    dtype, down = {"e4m3": (ml_dtypes.float8_e4m3fn, 7), "e5m2": (ml_dtypes.float8_e5m2, 14)}[fmt]
    v = np.moveaxis(np.asarray(x, np.float32).astype(ml_dtypes.bfloat16).astype(np.float64), axis, -1)
    blocks = v.reshape(v.shape[:-1] + (-1, 32))
    amax = np.abs(blocks).max(-1, keepdims=True)
    byte = np.maximum(np.where(amax > 0, np.frexp(amax)[1] - 1 + 127, 0) - down, 1)
    scale = np.exp2(byte - 127.0)
    codes = (blocks / scale).astype(np.float32).astype(dtype).astype(np.float64)
    return np.moveaxis((codes * scale).reshape(v.shape), -1, axis)


WIDE = False


def mx_kscale(k):
    if not WIDE:
        return np.ones(k)
    levels = np.array([10, -10, 5, -5, 0])
    if k % 512:
        return np.exp2(np.random.permutation(np.resize(levels, k // 32))).repeat(32)
    a = np.empty((k // 512, 16))
    for p in range(k // 512):
        a[p, :8] = np.random.permutation(np.resize(levels, 8))
        for g in range(8):
            far = levels[np.abs(levels - a[p, g]) >= 10]
            a[p, g + 8] = far[np.random.randint(len(far))]
    return np.exp2(a.ravel()).repeat(32)


def f64(x):
    return np.asarray(x).astype(np.float64)


def striped(idx):
    return np.tile(idx.reshape(-1, 16).T, (8, 1)).astype(np.uint16)


def unstriped(offs):
    return offs[:16].T.reshape(-1).astype(np.int64)


E2M1 = np.array([0.0, 0.5, 1.0, 1.5, 2.0, 3.0, 4.0, 6.0, -0.0, -0.5, -1.0, -1.5, -2.0, -3.0, -4.0, -6.0])


def pack_weight(w, fmt):
    k, n = w.shape
    w = f64(np.asarray(w, np.float32).astype(ml_dtypes.bfloat16)).reshape(k // 32, 32, n)
    amax = np.abs(w).max(1)
    if fmt == "e4m3":
        byte = np.frexp(amax)[1] - 1 + 127 - 7
    else:
        mant, ex = np.frexp(amax / 6.0)
        byte = np.where(mant > 0.5, ex, ex - 1) + 127
    byte = np.clip(np.where(amax > 0, byte, 1), 1, 254)
    scaled = (w * np.exp2(127.0 - byte)[:, None, :]).reshape(k, n).astype(np.float32)
    by_word = np.ascontiguousarray(scaled.reshape(k // 512, 128, 4, n).transpose(0, 1, 3, 2))
    if fmt == "e4m3":
        words = by_word.astype(ml_dtypes.float8_e4m3fn).view(np.uint8)
    else:
        c = by_word.astype(ml_dtypes.float4_e2m1fn).view(np.uint8) & 0xF
        words = (c[..., 0::2] | (c[..., 1::2] << 4)).reshape(k // 512, 128, 2 * n)
    return np.ascontiguousarray(words), np.ascontiguousarray(byte.astype(np.uint8).reshape(k // 512, 16, n))


def unpack_weight(words, scales, fmt):
    g, _, n = scales.shape
    words = np.ascontiguousarray(words).reshape(g, 128, n, -1)
    if fmt == "e4m3":
        vals = words.view(ml_dtypes.float8_e4m3fn).astype(np.float64)
    else:
        nib = np.empty((g, 128, n, 4), np.uint8)
        nib[..., 0::2] = words & 0xF
        nib[..., 1::2] = words >> 4
        vals = E2M1[nib]
    vals = vals * np.repeat(np.exp2(scales.astype(np.float64) - 127.0), 8, axis=1)[..., None]
    return vals.transpose(0, 1, 3, 2).reshape(g * 512, n)


def gelu(v):
    return 0.5 * v * (1.0 + np.tanh(np.sqrt(2.0 / np.pi) * (v + 0.044715 * v**3)))


def bf(x):
    return np.asarray(x, np.float32).astype(ml_dtypes.bfloat16)


def planes(Y):
    n, m = Y.shape
    b = f64(bf(Y)).reshape(n // 32, 32, m)
    amax = np.abs(b).max(1)
    byte = np.clip(np.where(amax > 0, np.frexp(amax)[1] - 1 + 127 - 7, 1), 1, 254)
    codes = (b * np.exp2(127.0 - byte)[:, None, :]).reshape(n, m).astype(np.float32).astype(ml_dtypes.float8_e4m3fn).view(np.uint8)
    words = codes.reshape(n // 512, 128, 4, m).transpose(0, 1, 3, 2)
    return np.ascontiguousarray(words), np.ascontiguousarray(byte.astype(np.uint8).reshape(n // 512, 16, m))


K, T, S, H, N = 1536, 2048, 1024, 512, 1024

def setup_inputs():
    n = np.random.standard_normal
    s = mx_kscale(K)[:, None]
    u = mx_kscale(H)[:, None]
    ru = np.sqrt(u)
    g = np.exp(0.8 * n(N))[None, :]
    tab_words, tab_scales = pack_weight(n((K, T)) * s, "e4m3")
    w4_words, w4_scales = pack_weight(0.7 * n((K, H)) / np.sqrt(K) / s * ru.T, "e2m1")
    return {
        "tab_words": tab_words, "tab_scales": tab_scales,
        "offs": striped(np.random.permutation(T)[:S]),
        "w1": (0.7 * n((K, H)) / np.sqrt(K) / s * ru.T).astype(np.float32),
        "w4_words": w4_words, "w4_scales": w4_scales,
        "spin": (n((H, S)) * u).astype(np.float32),
        "w3": (0.25 * n((H, N)) / np.sqrt(H) / u * g).astype(np.float32),
        "offs2": striped(np.random.permutation(S)),
        "wgo": np.exp(0.3 * n((128, S))).astype(np.float32),
        "x0": (0.5 * n((N, S)) * g.T).astype(np.float32),
    }

def reference(tab_words, tab_scales, offs, w1, w4_words, w4_scales, spin, w3, offs2, wgo, x0):
    v = unpack_weight(tab_words, tab_scales, "e4m3")[:, unstriped(offs)]
    W1 = mxq(f64(w1), 0, "e4m3")
    W4 = unpack_weight(w4_words, w4_scales, "e2m1")
    d = (W1.T @ v) - (W4.T @ v)
    h = np.square(d) + f64(spin)
    corr = mxq(f64(w3), 0, "e4m3").T @ mxq(h, 0, "e4m3")
    page = np.zeros((N, S))
    page[:, unstriped(offs2)] = np.tile(f64(wgo), (N // 128, 1)) * corr
    gate = 1 / (1 + np.exp(-page))
    y = (page - f64(x0)) * gate
    words, scales = planes(y)
    return y, words, scales

@@ -1,0 +1,335 @@
+from contextlib import ExitStack
+
+import concourse.mybir as mybir
+from concourse.masks import make_identity
+
+K, T, S, H, N = 1536, 2048, 1024, 512, 1024
+FLOPS = 2 * (2 * K * H * S + H * N * S)
+
+F32 = mybir.dt.float32
+BF16 = mybir.dt.bfloat16
+I32 = mybir.dt.int32
+U32 = mybir.dt.uint32
+U16 = mybir.dt.uint16
+U8 = mybir.dt.uint8
+FP8X4 = mybir.dt.float8_e4m3fn_x4
+FP4X4 = mybir.dt.float4_e2m1fn_x4
+ACT = mybir.ActivationFunctionType
+ALU = mybir.AluOpType
+
+P = 128
+PACK = 4
+K_PASS = P * PACK
+PASSES = K // K_PASS
+GROUPS = N // K_PASS
+HALF = 512
+HALVES = S // HALF
+LIST_COLS = HALF // 16
+QUADS = 4
+PAGE_COLS = 1408
+SLICES = GROUPS * PACK
+
+
+def tile_list_tube_reading_correction_kernel(
+    tc, tab_words, tab_scales, offs, w1, w4_words, w4_scales, spin, w3, offs2, wgo, x0, out_0, out_1, out_2
+):
+    nc = tc.nc
+    with ExitStack() as ctx:
+        keep = ctx.enter_context(tc.tile_pool(name="keep", bufs=1))
+        ring = ctx.enter_context(tc.tile_pool(name="ring", bufs=2))
+        psum = ctx.enter_context(tc.psum_pool(name="psum", bufs=1))
+
+        def bank(k):
+            return psum.tile([P, HALF], F32, name="bank%d" % k, tag="bank%d" % k)
+
+        def cols(c):
+            return slice(c * HALF, (c + 1) * HALF)
+
+        pick = keep.tile([P, S // 16], U16, name="pick")
+        nc.sync.dma_start(pick[:], offs)
+
+        def load_scale_rows(scales, width, name):
+            stacked = keep.tile([P, width], U8, name=name, align_bytes=64)
+            nc.sync.dma_start(stacked[16:64, :].bitcast(I32), scales.bitcast(I32).rearrange("a q t -> q a t"))
+            nc.vector.memset(stacked[0:16, :].bitcast(I32), 0)
+            nc.vector.memset(stacked[64:P, :].bitcast(I32), 0)
+            return stacked
+
+        def spread_scale_rows(stacked, width, name):
+            spread = keep.tile([P, PASSES * width], U8, name=name, align_bytes=64)
+            for q in range(QUADS):
+                nc.gpsimd.dma_start(
+                    spread[32 * q : 32 * q + 4, :].bitcast(I32).rearrange("r (a t) -> r a t", a=PASSES),
+                    stacked[16 + 12 * q : 28 + 12 * q, :].bitcast(I32),
+                )
+            return spread
+
+        tab_s = load_scale_rows(tab_scales, T, "tab_s")
+        w4_s_raw = load_scale_rows(w4_scales, H, "w4_s_raw")
+
+        w4_raw = keep.tile([P, PASSES * 2 * H], U8, name="w4_raw", align_bytes=64)
+        nc.sync.dma_start(
+            w4_raw[:].bitcast(I32).rearrange("p (a c) -> p a c", a=PASSES),
+            w4_words.bitcast(I32).rearrange("a p c -> p a c"),
+        )
+
+        def load_table(a):
+            words = keep.tile([P, T], U32, name="tab_w%d" % a, align_bytes=64)
+            nc.sync.dma_start(words[:].bitcast(I32), tab_words[a].rearrange("p t i -> p (t i)").bitcast(I32))
+            return words
+
+        def load_rows(rows):
+            raw = ring.tile([P, PACK, HALF], F32, name="raw", tag="raw", bufs=4, align_bytes=64)
+            nc.sync.dma_start(raw[:], rows)
+            return raw
+
+        def quantize_weight(raw, sign, name):
+            dealt = ring.tile([P, PACK * HALF], BF16, name="dealt", tag="bf", bufs=3, align_bytes=64)
+            nc.scalar.activation(
+                dealt[:].rearrange("p (t m j) -> p m j t", t=PACK, j=PACK),
+                raw[:].rearrange("p j (m t) -> p m j t", t=PACK),
+                ACT.Copy,
+                scale=sign,
+            )
+            codes = keep.tile([P, HALF], U32, name=name + "_codes", align_bytes=64)
+            scales = keep.tile([P, HALF], U8, name=name + "_scales", align_bytes=64)
+            nc.vector.quantize_mx(out=codes[:].bitcast(FP8X4), scales=scales[:], in_=dealt[:])
+            return codes, scales
+
+        w1_rows = w1.rearrange("(a p j) r -> a p j r", p=P, j=PACK)
+        w3_rows = w3.rearrange("(p j) n -> p j n", j=PACK)
+        spin_rows = spin.rearrange("(p t) j -> p t j", t=PACK)
+        x0_rows = x0.rearrange("(g p t) m -> g p t m", p=P, t=PACK)
+        y_rows = out_0.rearrange("(g p t) m -> g p t m", p=P, t=PACK)
+        wgo_rows = wgo.rearrange("(m t) j -> m t j", t=PACK)
+
+        tab_w = [load_table(0)]
+        w1_raw = [load_rows(w1_rows[0])]
+        tab_w.append(load_table(1))
+        w1_raw.append(load_rows(w1_rows[1]))
+        w1_raw.append(load_rows(w1_rows[2]))
+        w3_raw = [load_rows(w3_rows[:, :, cols(0)])]
+        tab_w.append(load_table(2))
+        spin_sb = []
+        for c in range(HALVES):
+            sp = ring.tile([P, PACK, HALF], F32, name="spin_sb", tag="spin", bufs=2, align_bytes=64)
+            spin_sb.append(sp)
+        nc.sync.dma_start(spin_sb[0][:], spin_rows[:, :, cols(0)])
+        place = keep.tile([P, S // 16], U16, name="place")
+        nc.sync.dma_start(place[:], offs2)
+        wgo_sb = keep.tile([P, PACK, S], F32, name="wgo_sb")
+
+        def load_wgo(c):
+            for q in range(QUADS):
+                nc.sync.dma_start(wgo_sb[32 * q : 32 * q + 32, :, cols(c)], wgo_rows[:, :, cols(c)])
+
+        load_wgo(0)
+        nc.sync.dma_start(spin_sb[1][:], spin_rows[:, :, cols(1)])
+
+        ident = keep.tile([P, P], F32, name="ident")
+        make_identity(nc, ident[:])
+
+        v_s_stacked = keep.tile([P, S], U8, name="v_s_stacked", align_bytes=64)
+        nc.vector.tensor_copy(v_s_stacked[:], tab_s[:].indirect(pick[:]))
+        joined = keep.tile([P, S + H], U8, name="joined", align_bytes=64)
+        nc.vector.tensor_copy(
+            joined[:, S : S + H].rearrange("p (t m) -> p t m", t=PACK),
+            w4_s_raw[:].rearrange("p (m t) -> p t m", t=PACK),
+        )
+        nc.vector.tensor_copy(joined[:, 0:S].bitcast(I32), v_s_stacked[:].bitcast(I32))
+        planes_in = spread_scale_rows(joined, S + H, "planes_in")
+
+        w4_c = keep.tile([P, PASSES * 2 * H], U8, name="w4_c", align_bytes=64)
+        nc.vector.tensor_copy(
+            w4_c[:].bitcast(U16).rearrange("p (a t m) -> p a t m", a=PASSES, t=PACK),
+            w4_raw[:].bitcast(U16).rearrange("p (a m t) -> p a t m", a=PASSES, t=PACK),
+        )
+
+        w1_q = []
+        w3_q = []
+        v_w = {}
+        for a in range(PASSES):
+            w1_q.append(quantize_weight(w1_raw[a], -1.0, "w1_%d" % a))
+            if a == PASSES - 1:
+                w3_q.append(quantize_weight(w3_raw[0], 1.0, "w3_0"))
+            for c in range(HALVES):
+                words = keep.tile([P, HALF], U32, name="v_w%d_%d" % (a, c), align_bytes=64)
+                nc.vector.tensor_copy(words[:], tab_w[a][:].indirect(pick[:, c * LIST_COLS : (c + 1) * LIST_COLS]))
+                v_w.setdefault((a, c), words)
+
+        w3_raw.append(load_rows(w3_rows[:, :, cols(1)]))
+        x0_sb = []
+
+        def load_x0(g):
+            for u in range(2):
+                pair = ring.tile([P, 2, S], F32, name="x0_pair", tag="raw", bufs=4, align_bytes=64)
+                nc.sync.dma_start(pair[:], x0_rows[g][:, 2 * u : 2 * u + 2, :])
+                x0_sb.extend([pair[:, 0, :], pair[:, 1, :]])
+
+        load_wgo(1)
+        load_x0(0)
+
+        h_q = []
+
+        def hidden(c):
+            d_bank = [bank(PACK * c + t) for t in range(PACK)]
+            for a in range(PASSES):
+                moving = v_w[(a, c)][:].bitcast(FP8X4)
+                base = a * (S + H)
+                moving_s = planes_in[:, base + c * HALF : base + (c + 1) * HALF]
+                for t in range(PACK):
+                    nc.tensor.matmul_mx(
+                        out=d_bank[t][:],
+                        lhsT=w4_c[:, 2 * (a * H + t * P) : 2 * (a * H + (t + 1) * P)].bitcast(FP4X4),
+                        lhsT_scale=planes_in[:, base + S + t * P : base + S + (t + 1) * P],
+                        rhs=moving,
+                        rhs_scale=moving_s,
+                        start=(a == 0),
+                        stop=False,
+                    )
+                    nc.tensor.matmul_mx(
+                        out=d_bank[t][:],
+                        lhsT=w1_q[a][0][:, t * P : (t + 1) * P].bitcast(FP8X4),
+                        lhsT_scale=w1_q[a][1][:, t * P : (t + 1) * P],
+                        rhs=moving,
+                        rhs_scale=moving_s,
+                        start=False,
+                        stop=(a == PASSES - 1),
+                    )
+            sq = ring.tile([P, PACK, HALF], F32, name="sq", tag="sq", bufs=2, align_bytes=64)
+            for t in range(PACK):
+                nc.scalar.activation(sq[:, t, :], d_bank[t][:], ACT.Square)
+            h_bf = ring.tile([P, PACK * HALF], BF16, name="h_bf", tag="bf", bufs=3, align_bytes=64)
+            nc.vector.tensor_tensor(
+                h_bf[:].rearrange("p (c i t) -> p c t i", i=4, t=PACK),
+                sq[:].rearrange("p t (c i) -> p c t i", i=4),
+                spin_sb[c][:].rearrange("p t (c i) -> p c t i", i=4),
+                ALU.add,
+            )
+            h_c = keep.tile([P, HALF], U32, name="h_c%d" % c, align_bytes=64)
+            h_s = keep.tile([P, HALF], U8, name="h_s%d" % c, align_bytes=64)
+            nc.vector.quantize_mx(out=h_c[:].bitcast(FP8X4), scales=h_s[:], in_=h_bf[:])
+            h_q.append((h_c, h_s))
+
+        rows = keep.tile([P, (SLICES + 1) * S], F32, name="rows")
+
+        def corr_cols(i, c):
+            return slice(i * S + c * HALF, i * S + (c + 1) * HALF)
+
+        def correct(i, c, k):
+            g, t = divmod(i, PACK)
+            acc = bank(k)
+            nc.tensor.matmul_mx(
+                out=acc[:],
+                lhsT=w3_q[g][0][:, t * P : (t + 1) * P].bitcast(FP8X4),
+                lhsT_scale=w3_q[g][1][:, t * P : (t + 1) * P],
+                rhs=h_q[c][0][:].bitcast(FP8X4),
+                rhs_scale=h_q[c][1][:],
+                start=True,
+                stop=True,
+            )
+            nc.scalar.activation(rows[:, corr_cols(i, c)], acc[:], ACT.Copy, scale=-1.0)
+
+        def new_page():
+            return ring.tile([P, PAGE_COLS], F32, name="page", tag="page", bufs=3)
+
+        def scatter_half(page, i, c):
+            nc.vector.tensor_tensor(
+                page[:].indirect(place[:, c * LIST_COLS : (c + 1) * LIST_COLS]),
+                rows[:, corr_cols(i, c)],
+                wgo_sb[:, i % PACK, cols(c)],
+                ALU.mult,
+            )
+
+        def scatter_whole(page, i):
+            nc.vector.tensor_tensor(
+                page[:].indirect(place[:]), rows[:, i * S : (i + 1) * S], wgo_sb[:, i % PACK, :], ALU.mult
+            )
+
+        def finish(page, i):
+            g, t = divmod(i, PACK)
+            gate = ring.tile([P, S], F32, name="gate", tag="gate", bufs=2)
+            y = rows[:, (i + 1) * S : (i + 2) * S]
+            if i == SLICES - 1:
+                dev = ring.tile([P, S], F32, name="dev", tag="sq", bufs=2, align_bytes=64)
+                for c in range(HALVES):
+                    nc.scalar.activation(gate[:, cols(c)], page[:, cols(c)], ACT.Sigmoid, scale=-1.0)
+                    nc.vector.scalar_tensor_tensor(
+                        dev[:, cols(c)], page[:, cols(c)], -1.0, x0_sb[i][:, cols(c)], ALU.mult, ALU.subtract
+                    )
+                for c in range(HALVES):
+                    nc.vector.tensor_tensor(y[:, cols(c)], dev[:, cols(c)], gate[:, cols(c)], ALU.mult)
+                    nc.sync.dma_start(y_rows[g][:, t, cols(c)], y[:, cols(c)])
+                return
+            nc.scalar.activation(gate[:], page[:, 0:S], ACT.Sigmoid, scale=-1.0)
+            turned = ring.tile([P, S], F32, name="turned", tag="sq", bufs=2, align_bytes=64)
+            for c in range(HALVES):
+                acc = bank(4 + c)
+                for b in range(4):
+                    blk = slice(c * HALF + b * P, c * HALF + (b + 1) * P)
+                    nc.tensor.matmul(
+                        acc[:, b * P : (b + 1) * P], x0_sb[i][:, blk], ident[:], start=True, stop=False, is_transpose=True
+                    )
+                    nc.tensor.matmul(
+                        acc[:, b * P : (b + 1) * P], page[:, blk], ident[:], start=False, stop=True, is_transpose=True
+                    )
+                nc.scalar.activation(turned[:, cols(c)], acc[:], ACT.Copy, scale=-1.0)
+            for c in range(HALVES):
+                acc = bank(6 + c)
+                for b in range(4):
+                    blk = slice(c * HALF + b * P, c * HALF + (b + 1) * P)
+                    nc.tensor.transpose(acc[:, b * P : (b + 1) * P], turned[:, blk], ident[:])
+                nc.vector.tensor_tensor(y[:, cols(c)], acc[:], gate[:, cols(c)], ALU.mult)
+            nc.sync.dma_start(y_rows[g][:, t, :], y)
+
+        def planes(g):
+            y4 = rows[:, (PACK * g + 1) * S : (PACK * g + PACK + 1) * S].rearrange("p (t m) -> p t m", t=PACK)
+            y_bf = ring.tile([P, PACK * S], BF16, name="y_bf", tag="spin", bufs=2, align_bytes=64)
+            y_c = keep.tile([P, S], U32, name="y_c%d" % g, align_bytes=64)
+            y_s = keep.tile([P, S], U8, name="y_s%d" % g, align_bytes=64)
+            width = S // 4
+            for k in range(4):
+                dst = y_bf[:, PACK * k * width : PACK * (k + 1) * width].rearrange("p (c i t) -> p c t i", i=4, t=PACK)
+                src = y4[:, :, k * width : (k + 1) * width].rearrange("p t (c i) -> p c t i", i=4)
+                if g == GROUPS - 1 and k % 2 == 0:
+                    nc.vector.tensor_copy(dst, src)
+                else:
+                    nc.scalar.copy(dst, src)
+            words_out = out_1[g].rearrange("p m t -> p (m t)").bitcast(I32)
+            for c in range(HALVES):
+                nc.vector.quantize_mx(
+                    out=y_c[:, cols(c)].bitcast(FP8X4),
+                    scales=y_s[:, cols(c)],
+                    in_=y_bf[:, PACK * c * HALF : PACK * (c + 1) * HALF],
+                )
+                nc.sync.dma_start(words_out[:, cols(c)], y_c[:, cols(c)].bitcast(I32))
+            for q in range(QUADS):
+                eng = nc.scalar if g == GROUPS - 1 and q % 2 == 1 else nc.sync
+                eng.dma_start(out_2[g, 4 * q : 4 * q + 4, :].bitcast(I32), y_s[32 * q : 32 * q + 4, :].bitcast(I32))
+
+        pages = [new_page() for i in range(3)]
+        hidden(0)
+        for i in range(2):
+            correct(i, 0, i)
+        for i in range(2):
+            scatter_half(pages[i], i, 0)
+        hidden(1)
+        order = [(2, 0), (0, 1), (1, 1), (2, 1)] + [(i, c) for i in range(3, SLICES) for c in range(HALVES)]
+        for n, (i, c) in enumerate(order):
+            if (i, c) == (PACK, 0):
+                w3_q.append(quantize_weight(w3_raw[1], 1.0, "w3_1"))
+                load_x0(1)
+            correct(i, c, (n + 2) % PACK)
+        scatter_half(pages[2], 2, 0)
+        for i in range(3):
+            scatter_half(pages[i], i, 1)
+        finish(pages[0], 0)
+        finish(pages[1], 1)
+        for i in range(3, SLICES):
+            pages.append(new_page())
+            scatter_whole(pages[i], i)
+            finish(pages[i - 1], i - 1)
+            if i - 1 == PACK:
+                planes(0)
+        finish(pages[SLICES - 1], SLICES - 1)
+        planes(1)

@@ -28,6 +28,10 @@ LIST_COLS = HALF // 16
 QUADS = 4
 PAGE_COLS = 1408
 SLICES = GROUPS * PACK
+EARLY = 3
+TURNED = 7
+VECTOR_SHARE = 80
+W3_SHARE = 128
 
 
 def tile_list_tube_reading_correction_kernel(
@@ -45,8 +49,12 @@ def tile_list_tube_reading_correction_kernel(
         def cols(c):
             return slice(c * HALF, (c + 1) * HALF)
 
-        pick = keep.tile([P, S // 16], U16, name="pick")
-        nc.sync.dma_start(pick[:], offs)
+        w1_rows = w1.rearrange("(a p j) r -> a p j r", p=P, j=PACK)
+        w3_rows = w3.rearrange("(p j) n -> p j n", j=PACK)
+        spin_rows = spin.rearrange("(p t) j -> p t j", t=PACK)
+        x0_rows = x0.rearrange("(g p t) m -> g p t m", p=P, t=PACK)
+        y_rows = out_0.rearrange("(g p t) m -> g p t m", p=P, t=PACK)
+        wgo_rows = wgo.rearrange("(m t) j -> m t j", t=PACK)
 
         def load_scale_rows(scales, width, name):
             stacked = keep.tile([P, width], U8, name=name, align_bytes=64)
@@ -55,89 +63,83 @@ def tile_list_tube_reading_correction_kernel(
             nc.vector.memset(stacked[64:P, :].bitcast(I32), 0)
             return stacked
 
-        def spread_scale_rows(stacked, width, name):
-            spread = keep.tile([P, PASSES * width], U8, name=name, align_bytes=64)
-            for q in range(QUADS):
-                nc.gpsimd.dma_start(
-                    spread[32 * q : 32 * q + 4, :].bitcast(I32).rearrange("r (a t) -> r a t", a=PASSES),
-                    stacked[16 + 12 * q : 28 + 12 * q, :].bitcast(I32),
-                )
-            return spread
-
-        tab_s = load_scale_rows(tab_scales, T, "tab_s")
-        w4_s_raw = load_scale_rows(w4_scales, H, "w4_s_raw")
-
-        w4_raw = keep.tile([P, PASSES * 2 * H], U8, name="w4_raw", align_bytes=64)
-        nc.sync.dma_start(
-            w4_raw[:].bitcast(I32).rearrange("p (a c) -> p a c", a=PASSES),
-            w4_words.bitcast(I32).rearrange("a p c -> p a c"),
-        )
-
         def load_table(a):
-            words = keep.tile([P, T], U32, name="tab_w%d" % a, align_bytes=64)
+            words = ring.tile([P, T], U32, name="tab_w", tag="wide", align_bytes=64)
             nc.sync.dma_start(words[:].bitcast(I32), tab_words[a].rearrange("p t i -> p (t i)").bitcast(I32))
             return words
 
-        def load_rows(rows):
-            raw = ring.tile([P, PACK, HALF], F32, name="raw", tag="raw", bufs=4, align_bytes=64)
+        def load_rows(rows, tag, name):
+            raw = ring.tile([P, PACK, HALF], F32, name=name, tag=tag, align_bytes=64)
             nc.sync.dma_start(raw[:], rows)
             return raw
 
-        def quantize_weight(raw, sign, name):
-            dealt = ring.tile([P, PACK * HALF], BF16, name="dealt", tag="bf", bufs=3, align_bytes=64)
-            nc.scalar.activation(
-                dealt[:].rearrange("p (t m j) -> p m j t", t=PACK, j=PACK),
-                raw[:].rearrange("p j (m t) -> p m j t", t=PACK),
-                ACT.Copy,
-                scale=sign,
-            )
+        def load_wgo(c, cuts):
+            part = ring.tile([P, PACK, HALF], F32, name="wgo_sb", tag="wide", align_bytes=64)
+            for first, last in cuts:
+                for q in (0, 2, 1, 3):
+                    nc.sync.dma_start(part[32 * q : 32 * q + 32, first:last, :], wgo_rows[:, first:last, cols(c)])
+            return [part[:, t, :] for t in range(PACK)]
+
+        def load_x0(g, u):
+            pair = ring.tile([P, 2, S], F32, name="x0_pair", tag="raw", align_bytes=64)
+            nc.sync.dma_start(pair[:], x0_rows[g][:, 2 * u : 2 * u + 2, :])
+            return [pair[:, 0, :], pair[:, 1, :]]
+
+        def quantize_weight(raw, sign, name, shared, tag="bf", bufs=2):
+            dealt = ring.tile([P, PACK * HALF], BF16, name="dealt", tag=tag, bufs=bufs, align_bytes=64)
+            dst = dealt[:].rearrange("p (t m j) -> p m j t", t=PACK, j=PACK)
+            src = raw[:].rearrange("p j (m t) -> p m j t", t=PACK)
+            if shared < P:
+                nc.scalar.activation(dst[:, shared:, :, :], src[:, shared:, :, :], ACT.Copy, scale=sign)
+            if shared:
+                nc.vector.tensor_scalar(dst[:, :shared, :, :], src[:, :shared, :, :], sign, None, ALU.mult)
             codes = keep.tile([P, HALF], U32, name=name + "_codes", align_bytes=64)
             scales = keep.tile([P, HALF], U8, name=name + "_scales", align_bytes=64)
             nc.vector.quantize_mx(out=codes[:].bitcast(FP8X4), scales=scales[:], in_=dealt[:])
             return codes, scales
 
-        w1_rows = w1.rearrange("(a p j) r -> a p j r", p=P, j=PACK)
-        w3_rows = w3.rearrange("(p j) n -> p j n", j=PACK)
-        spin_rows = spin.rearrange("(p t) j -> p t j", t=PACK)
-        x0_rows = x0.rearrange("(g p t) m -> g p t m", p=P, t=PACK)
-        y_rows = out_0.rearrange("(g p t) m -> g p t m", p=P, t=PACK)
-        wgo_rows = wgo.rearrange("(m t) j -> m t j", t=PACK)
+        def pick_words(words, a):
+            picked = []
+            for c in range(HALVES):
+                part = keep.tile([P, HALF], U32, name="v_w%d_%d" % (a, c), align_bytes=64)
+                nc.vector.tensor_copy(part[:], words[:].indirect(pick[:, c * LIST_COLS : (c + 1) * LIST_COLS]))
+                picked.append(part)
+            return picked
 
-        tab_w = [load_table(0)]
-        w1_raw = [load_rows(w1_rows[0])]
-        tab_w.append(load_table(1))
-        w1_raw.append(load_rows(w1_rows[1]))
-        w1_raw.append(load_rows(w1_rows[2]))
-        w3_raw = [load_rows(w3_rows[:, :, cols(0)])]
-        tab_w.append(load_table(2))
-        spin_sb = []
-        for c in range(HALVES):
-            sp = ring.tile([P, PACK, HALF], F32, name="spin_sb", tag="spin", bufs=2, align_bytes=64)
-            spin_sb.append(sp)
-        nc.sync.dma_start(spin_sb[0][:], spin_rows[:, :, cols(0)])
+        pick = keep.tile([P, S // 16], U16, name="pick")
+        nc.sync.dma_start(pick[:], offs)
+        tab_s = load_scale_rows(tab_scales, T, "tab_s")
+        w4_s_raw = load_scale_rows(w4_scales, H, "w4_s_raw")
+        w4_raw = keep.tile([P, PASSES * 2 * H], U8, name="w4_raw", align_bytes=64)
+        nc.sync.dma_start(
+            w4_raw[:].bitcast(I32).rearrange("p (a c) -> p a c", a=PASSES),
+            w4_words.bitcast(I32).rearrange("a p c -> p a c"),
+        )
+        tab_w = []
+        w1_raw = []
+        for a in range(2):
+            tab_w.append(load_table(a))
+            w1_raw.append(load_rows(w1_rows[a], "raw", "w1_raw"))
         place = keep.tile([P, S // 16], U16, name="place")
         nc.sync.dma_start(place[:], offs2)
-        wgo_sb = keep.tile([P, PACK, S], F32, name="wgo_sb")
-
-        def load_wgo(c):
-            for q in range(QUADS):
-                nc.sync.dma_start(wgo_sb[32 * q : 32 * q + 32, :, cols(c)], wgo_rows[:, :, cols(c)])
-
-        load_wgo(0)
-        nc.sync.dma_start(spin_sb[1][:], spin_rows[:, :, cols(1)])
 
         ident = keep.tile([P, P], F32, name="ident")
         make_identity(nc, ident[:])
 
-        v_s_stacked = keep.tile([P, S], U8, name="v_s_stacked", align_bytes=64)
-        nc.vector.tensor_copy(v_s_stacked[:], tab_s[:].indirect(pick[:]))
+        v_s = keep.tile([P, S], U8, name="v_s", align_bytes=64)
+        nc.vector.tensor_copy(v_s[:], tab_s[:].indirect(pick[:]))
         joined = keep.tile([P, S + H], U8, name="joined", align_bytes=64)
         nc.vector.tensor_copy(
             joined[:, S : S + H].rearrange("p (t m) -> p t m", t=PACK),
             w4_s_raw[:].rearrange("p (m t) -> p t m", t=PACK),
         )
-        nc.vector.tensor_copy(joined[:, 0:S].bitcast(I32), v_s_stacked[:].bitcast(I32))
-        planes_in = spread_scale_rows(joined, S + H, "planes_in")
+        nc.vector.tensor_copy(joined[:, 0:S].bitcast(I32), v_s[:].bitcast(I32))
+        given_s = keep.tile([P, PASSES * (S + H)], U8, name="given_s", align_bytes=64)
+        for q in range(QUADS):
+            nc.scalar.dma_start(
+                given_s[32 * q : 32 * q + 4, :].bitcast(I32).rearrange("r (a t) -> r a t", a=PASSES),
+                joined[16 + 12 * q : 28 + 12 * q, :].bitcast(I32),
+            )
 
         w4_c = keep.tile([P, PASSES * 2 * H], U8, name="w4_c", align_bytes=64)
         nc.vector.tensor_copy(
@@ -145,76 +147,78 @@ def tile_list_tube_reading_correction_kernel(
             w4_raw[:].bitcast(U16).rearrange("p (a m t) -> p a t m", a=PASSES, t=PACK),
         )
 
-        w1_q = []
-        w3_q = []
-        v_w = {}
-        for a in range(PASSES):
-            w1_q.append(quantize_weight(w1_raw[a], -1.0, "w1_%d" % a))
-            if a == PASSES - 1:
-                w3_q.append(quantize_weight(w3_raw[0], 1.0, "w3_0"))
-            for c in range(HALVES):
-                words = keep.tile([P, HALF], U32, name="v_w%d_%d" % (a, c), align_bytes=64)
-                nc.vector.tensor_copy(words[:], tab_w[a][:].indirect(pick[:, c * LIST_COLS : (c + 1) * LIST_COLS]))
-                v_w.setdefault((a, c), words)
+        v_w = [pick_words(tab_w[0], 0)]
+        tab_w.append(load_table(2))
+        w1_q = [quantize_weight(w1_raw[0], -1.0, "w1_0", 0)]
+        w1_raw.append(load_rows(w1_rows[2], "raw", "w1_raw"))
+        v_w.append(pick_words(tab_w[1], 1))
+        w3_raw = [load_rows(w3_rows[:, :, cols(0)], "wide", "w3_raw")]
+        w1_q.append(quantize_weight(w1_raw[1], -1.0, "w1_1", 0))
+        spin_sb = [load_rows(spin_rows[:, :, cols(0)], "raw", "spin_sb")]
+        v_w.append(pick_words(tab_w[2], 2))
+        wgo_sb = [load_wgo(0, [(0, 1), (1, PACK)])]
+        w1_q.append(quantize_weight(w1_raw[2], -1.0, "w1_2", VECTOR_SHARE))
+        spin_sb.append(load_rows(spin_rows[:, :, cols(1)], "raw", "spin_sb"))
 
-        w3_raw.append(load_rows(w3_rows[:, :, cols(1)]))
-        x0_sb = []
+        def difference(c, blocks):
+            width = HALF // blocks
+            d_bank = [bank(PACK * c + k) for k in range(PACK)]
 
-        def load_x0(g):
-            for u in range(2):
-                pair = ring.tile([P, 2, S], F32, name="x0_pair", tag="raw", bufs=4, align_bytes=64)
-                nc.sync.dma_start(pair[:], x0_rows[g][:, 2 * u : 2 * u + 2, :])
-                x0_sb.extend([pair[:, 0, :], pair[:, 1, :]])
+            def target(t, b):
+                if blocks == 1:
+                    return d_bank[t][:]
+                return d_bank[b][:, t * P : (t + 1) * P]
 
-        load_wgo(1)
-        load_x0(0)
-
-        h_q = []
-
-        def hidden(c):
-            d_bank = [bank(PACK * c + t) for t in range(PACK)]
             for a in range(PASSES):
-                moving = v_w[(a, c)][:].bitcast(FP8X4)
                 base = a * (S + H)
-                moving_s = planes_in[:, base + c * HALF : base + (c + 1) * HALF]
-                for t in range(PACK):
-                    nc.tensor.matmul_mx(
-                        out=d_bank[t][:],
-                        lhsT=w4_c[:, 2 * (a * H + t * P) : 2 * (a * H + (t + 1) * P)].bitcast(FP4X4),
-                        lhsT_scale=planes_in[:, base + S + t * P : base + S + (t + 1) * P],
-                        rhs=moving,
-                        rhs_scale=moving_s,
-                        start=(a == 0),
-                        stop=False,
-                    )
-                    nc.tensor.matmul_mx(
-                        out=d_bank[t][:],
-                        lhsT=w1_q[a][0][:, t * P : (t + 1) * P].bitcast(FP8X4),
-                        lhsT_scale=w1_q[a][1][:, t * P : (t + 1) * P],
-                        rhs=moving,
-                        rhs_scale=moving_s,
-                        start=False,
-                        stop=(a == PASSES - 1),
-                    )
-            sq = ring.tile([P, PACK, HALF], F32, name="sq", tag="sq", bufs=2, align_bytes=64)
-            for t in range(PACK):
-                nc.scalar.activation(sq[:, t, :], d_bank[t][:], ACT.Square)
-            h_bf = ring.tile([P, PACK * HALF], BF16, name="h_bf", tag="bf", bufs=3, align_bytes=64)
-            nc.vector.tensor_tensor(
-                h_bf[:].rearrange("p (c i t) -> p c t i", i=4, t=PACK),
-                sq[:].rearrange("p t (c i) -> p c t i", i=4),
-                spin_sb[c][:].rearrange("p t (c i) -> p c t i", i=4),
-                ALU.add,
-            )
+                for own in (False, True):
+                    for b in range(blocks):
+                        moving = v_w[a][c][:, b * width : (b + 1) * width].bitcast(FP8X4)
+                        first = base + c * HALF + b * width
+                        for t in range(PACK):
+                            if own:
+                                held = w1_q[a][0][:, t * P : (t + 1) * P].bitcast(FP8X4)
+                                held_s = w1_q[a][1][:, t * P : (t + 1) * P]
+                            else:
+                                held = w4_c[:, 2 * (a * H + t * P) : 2 * (a * H + (t + 1) * P)].bitcast(FP4X4)
+                                held_s = given_s[:, base + S + t * P : base + S + (t + 1) * P]
+                            nc.tensor.matmul_mx(
+                                out=target(t, b),
+                                lhsT=held,
+                                lhsT_scale=held_s,
+                                rhs=moving,
+                                rhs_scale=given_s[:, first : first + width],
+                                start=(a == 0 and not own and (blocks == 1 or t == 0)),
+                                stop=(a == PASSES - 1 and own and (blocks == 1 or t == PACK - 1)),
+                            )
+            sq = ring.tile([P, PACK * HALF], F32, name="sq", tag="sq", align_bytes=64)
+            for k in range(PACK):
+                nc.scalar.activation(sq[:, k * HALF : (k + 1) * HALF], d_bank[k][:], ACT.Square)
+            return sq
+
+        def hidden(c, sq, blocks):
+            width = HALF // blocks
+            h_bf = ring.tile([P, PACK * HALF], BF16, name="h_bf", tag="h_bf%d" % c, bufs=1, align_bytes=64)
+            for b in range(blocks):
+                part = slice(PACK * b * width, PACK * (b + 1) * width)
+                nc.vector.tensor_tensor(
+                    h_bf[:, part].rearrange("p (c i t) -> p c t i", i=4, t=PACK),
+                    sq[:, part].rearrange("p (t c i) -> p c t i", i=4, t=PACK),
+                    spin_sb[c][:, :, b * width : (b + 1) * width].rearrange("p t (c i) -> p c t i", i=4),
+                    ALU.add,
+                )
             h_c = keep.tile([P, HALF], U32, name="h_c%d" % c, align_bytes=64)
             h_s = keep.tile([P, HALF], U8, name="h_s%d" % c, align_bytes=64)
             nc.vector.quantize_mx(out=h_c[:].bitcast(FP8X4), scales=h_s[:], in_=h_bf[:])
-            h_q.append((h_c, h_s))
+            return h_c, h_s
 
-        rows = keep.tile([P, (SLICES + 1) * S], F32, name="rows")
+        rows = keep.tile([P, (SLICES + 0) * S], F32, name="rows")
 
-        def corr_cols(i, c):
-            return slice(i * S + c * HALF, i * S + (c + 1) * HALF)
+        def corr(i, c):
+            return rows[:, i * S + c * HALF : i * S + (c + 1) * HALF]
+
+        def sign(i):
+            return -1.0 if i < TURNED else 1.0
 
         def correct(i, c, k):
             g, t = divmod(i, PACK)
@@ -228,41 +232,47 @@ def tile_list_tube_reading_correction_kernel(
                 start=True,
                 stop=True,
             )
-            nc.scalar.activation(rows[:, corr_cols(i, c)], acc[:], ACT.Copy, scale=-1.0)
+            if (i, c) == (0, 0):
+                nc.vector.scalar_tensor_tensor(corr(i, c), acc[:], sign(i), wgo_sb[c][t], ALU.mult, ALU.mult)
+                return
+            nc.scalar.activation(corr(i, c), acc[:], ACT.Copy, scale=sign(i))
+            nc.gpsimd.tensor_tensor(corr(i, c), corr(i, c), wgo_sb[c][t], ALU.mult)
 
-        def new_page():
+        def new_page(i):
+            if i == SLICES - 1:
+                return ring.tile([P, PAGE_COLS], F32, name="page", tag="y_bf0", bufs=1, align_bytes=64)
+            if i == EARLY - 1:
+                return ring.tile([P, PAGE_COLS], F32, name="page", tag="h_bf1", bufs=1, align_bytes=64)
             return ring.tile([P, PAGE_COLS], F32, name="page", tag="page", bufs=3)
 
-        def scatter_half(page, i, c):
-            nc.vector.tensor_tensor(
-                page[:].indirect(place[:, c * LIST_COLS : (c + 1) * LIST_COLS]),
-                rows[:, corr_cols(i, c)],
-                wgo_sb[:, i % PACK, cols(c)],
-                ALU.mult,
-            )
+        def scatter(i, c):
+            window = pages[i][:].indirect(place[:, c * LIST_COLS : (c + 1) * LIST_COLS])
+            nc.vector.tensor_copy(window, corr(i, c))
 
-        def scatter_whole(page, i):
-            nc.vector.tensor_tensor(
-                page[:].indirect(place[:]), rows[:, i * S : (i + 1) * S], wgo_sb[:, i % PACK, :], ALU.mult
-            )
+        def scatter_whole(i):
+            nc.vector.tensor_copy(pages[i][:].indirect(place[:]), rows[:, i * S : (i + 1) * S])
 
-        def finish(page, i):
+        def finish(i):
             g, t = divmod(i, PACK)
+            page = pages[i]
             gate = ring.tile([P, S], F32, name="gate", tag="gate", bufs=2)
-            y = rows[:, (i + 1) * S : (i + 2) * S]
+            y = rows[:, (i + 0) * S : (i + 1) * S]
             if i == SLICES - 1:
-                dev = ring.tile([P, S], F32, name="dev", tag="sq", bufs=2, align_bytes=64)
+                dev = ring.tile([P, S], F32, name="dev", tag="sq", align_bytes=64)
                 for c in range(HALVES):
-                    nc.scalar.activation(gate[:, cols(c)], page[:, cols(c)], ACT.Sigmoid, scale=-1.0)
-                    nc.vector.scalar_tensor_tensor(
-                        dev[:, cols(c)], page[:, cols(c)], -1.0, x0_sb[i][:, cols(c)], ALU.mult, ALU.subtract
-                    )
+                    nc.scalar.activation(gate[:, cols(c)], page[:, cols(c)], ACT.Sigmoid)
+                    nc.vector.tensor_tensor(dev[:, cols(c)], page[:, cols(c)], x0_sb[i][:, cols(c)], ALU.subtract)
                 for c in range(HALVES):
                     nc.vector.tensor_tensor(y[:, cols(c)], dev[:, cols(c)], gate[:, cols(c)], ALU.mult)
                     nc.sync.dma_start(y_rows[g][:, t, cols(c)], y[:, cols(c)])
                 return
-            nc.scalar.activation(gate[:], page[:, 0:S], ACT.Sigmoid, scale=-1.0)
-            turned = ring.tile([P, S], F32, name="turned", tag="sq", bufs=2, align_bytes=64)
+            nc.scalar.activation(gate[:], page[:, 0:S], ACT.Sigmoid, scale=sign(i))
+            if i >= TURNED:
+                nc.gpsimd.tensor_tensor(y, page[:, 0:S], x0_sb[i], ALU.subtract)
+                nc.gpsimd.tensor_tensor(y, y, gate[:], ALU.mult)
+                nc.sync.dma_start(y_rows[g][:, t, :], y)
+                return
+            turned = ring.tile([P, S], F32, name="turned", tag="sq", align_bytes=64)
             for c in range(HALVES):
                 acc = bank(4 + c)
                 for b in range(4):
@@ -279,24 +289,21 @@ def tile_list_tube_reading_correction_kernel(
                 for b in range(4):
                     blk = slice(c * HALF + b * P, c * HALF + (b + 1) * P)
                     nc.tensor.transpose(acc[:, b * P : (b + 1) * P], turned[:, blk], ident[:])
-                nc.vector.tensor_tensor(y[:, cols(c)], acc[:], gate[:, cols(c)], ALU.mult)
+                nc.scalar.copy(y[:, cols(c)], acc[:])
+            nc.gpsimd.tensor_tensor(y, y, gate[:], ALU.mult)
             nc.sync.dma_start(y_rows[g][:, t, :], y)
 
-        def planes(g):
-            y4 = rows[:, (PACK * g + 1) * S : (PACK * g + PACK + 1) * S].rearrange("p (t m) -> p t m", t=PACK)
-            y_bf = ring.tile([P, PACK * S], BF16, name="y_bf", tag="spin", bufs=2, align_bytes=64)
+        def round_rows(y_bf, g, first, last, c, engine):
+            y4 = rows[:, PACK * g * S : PACK * (g + 1) * S].rearrange("p (t m) -> p t m", t=PACK)
+            dst = y_bf[:, PACK * c.start : PACK * c.stop].rearrange("p (c i t) -> p c t i", i=4, t=PACK)
+            src = y4[:, :, c].rearrange("p t (c i) -> p c t i", i=4)
+            engine(dst[:, :, first:last, :], src[:, :, first:last, :])
+
+        def planes(y_bf, g):
             y_c = keep.tile([P, S], U32, name="y_c%d" % g, align_bytes=64)
             y_s = keep.tile([P, S], U8, name="y_s%d" % g, align_bytes=64)
-            width = S // 4
-            for k in range(4):
-                dst = y_bf[:, PACK * k * width : PACK * (k + 1) * width].rearrange("p (c i t) -> p c t i", i=4, t=PACK)
-                src = y4[:, :, k * width : (k + 1) * width].rearrange("p t (c i) -> p c t i", i=4)
-                if g == GROUPS - 1 and k % 2 == 0:
-                    nc.vector.tensor_copy(dst, src)
-                else:
-                    nc.scalar.copy(dst, src)
             words_out = out_1[g].rearrange("p m t -> p (m t)").bitcast(I32)
-            for c in range(HALVES):
+            for c in (1, 0):
                 nc.vector.quantize_mx(
                     out=y_c[:, cols(c)].bitcast(FP8X4),
                     scales=y_s[:, cols(c)],
@@ -307,29 +314,42 @@ def tile_list_tube_reading_correction_kernel(
                 eng = nc.scalar if g == GROUPS - 1 and q % 2 == 1 else nc.sync
                 eng.dma_start(out_2[g, 4 * q : 4 * q + 4, :].bitcast(I32), y_s[32 * q : 32 * q + 4, :].bitcast(I32))
 
-        pages = [new_page() for i in range(3)]
-        hidden(0)
-        for i in range(2):
+        pages = [new_page(i) for i in range(EARLY - 1)]
+        w3_q = [quantize_weight(w3_raw[0], 1.0, "w3_0", W3_SHARE)]
+        wgo_sb.append(load_wgo(1, [(0, PACK)]))
+        h_q = [hidden(0, difference(0, PACK), PACK)]
+        w3_raw.append(load_rows(w3_rows[:, :, cols(1)], "raw", "w3_raw"))
+        for i in range(EARLY - 1):
             correct(i, 0, i)
-        for i in range(2):
-            scatter_half(pages[i], i, 0)
-        hidden(1)
-        order = [(2, 0), (0, 1), (1, 1), (2, 1)] + [(i, c) for i in range(3, SLICES) for c in range(HALVES)]
+            scatter(i, 0)
+        h_q.append(hidden(1, difference(1, 1), 1))
+        pages.append(new_page(EARLY - 1))
+        x0_sb = load_x0(0, 0)
+        order = [(EARLY - 1, 0)] + [(i, 1) for i in range(EARLY)]
+        order = order + [(i, c) for i in range(EARLY, SLICES) for c in range(HALVES)]
         for n, (i, c) in enumerate(order):
             if (i, c) == (PACK, 0):
-                w3_q.append(quantize_weight(w3_raw[1], 1.0, "w3_1"))
-                load_x0(1)
-            correct(i, c, (n + 2) % PACK)
-        scatter_half(pages[2], 2, 0)
-        for i in range(3):
-            scatter_half(pages[i], i, 1)
-        finish(pages[0], 0)
-        finish(pages[1], 1)
-        for i in range(3, SLICES):
-            pages.append(new_page())
-            scatter_whole(pages[i], i)
-            finish(pages[i - 1], i - 1)
-            if i - 1 == PACK:
-                planes(0)
-        finish(pages[SLICES - 1], SLICES - 1)
-        planes(1)
+                w3_q.append(quantize_weight(w3_raw[1], 1.0, "w3_1", 0, "h_bf0", 1))
+                x0_sb.extend(load_x0(0, 1))
+            correct(i, c, (n + EARLY - 1) % PACK)
+        for i, c in order[: EARLY + 1]:
+            scatter(i, c)
+        y_bf = [ring.tile([P, PACK * S], BF16, name="y_bf", tag="y_bf%d" % g, bufs=1, align_bytes=64) for g in range(GROUPS)]
+        for i in range(SLICES):
+            if i == SLICES - 2:
+                planes(y_bf[0], 0)
+            if EARLY <= i + 1 < SLICES:
+                pages.append(new_page(i + 1))
+                scatter_whole(i + 1)
+            finish(i)
+            if i in (1, 3):
+                x0_sb.extend(load_x0(1, i // 2))
+            if i == PACK:
+                for k in range(4):
+                    round_rows(y_bf[0], 0, 0, PACK, slice(k * S // 4, (k + 1) * S // 4), nc.scalar.copy)
+            if i == SLICES - 2:
+                for c in range(HALVES):
+                    round_rows(y_bf[1], 1, 0, 2, cols(c), nc.scalar.copy)
+        round_rows(y_bf[1], 1, 2, 4, cols(0), nc.scalar.copy)
+        round_rows(y_bf[1], 1, 2, 4, cols(1), nc.vector.tensor_copy)
+        planes(y_bf[1], 1)

@@ -28,9 +28,9 @@ LIST_COLS = HALF // 16
 QUADS = 4
 PAGE_COLS = 1408
 SLICES = GROUPS * PACK
-EARLY = 3
-TURNED = 7
-VECTOR_SHARE = 80
+EARLY = 4
+TURNED = 0
+VECTOR_SHARE = 72
 W3_SHARE = 128
 
 
@@ -63,25 +63,24 @@ def tile_list_tube_reading_correction_kernel(
             nc.vector.memset(stacked[64:P, :].bitcast(I32), 0)
             return stacked
 
-        def load_table(a):
-            words = ring.tile([P, T], U32, name="tab_w", tag="wide", align_bytes=64)
+        def load_table(a, tag):
+            words = ring.tile([P, T], U32, name="tab_w", tag=tag, bufs=1, align_bytes=64)
             nc.sync.dma_start(words[:].bitcast(I32), tab_words[a].rearrange("p t i -> p (t i)").bitcast(I32))
             return words
 
         def load_rows(rows, tag, name):
-            raw = ring.tile([P, PACK, HALF], F32, name=name, tag=tag, align_bytes=64)
+            raw = ring.tile([P, PACK, HALF], F32, name=name, tag=tag, bufs=1, align_bytes=64)
             nc.sync.dma_start(raw[:], rows)
             return raw
 
-        def load_wgo(c, cuts):
-            part = ring.tile([P, PACK, HALF], F32, name="wgo_sb", tag="wide", align_bytes=64)
-            for first, last in cuts:
-                for q in (0, 2, 1, 3):
-                    nc.sync.dma_start(part[32 * q : 32 * q + 32, first:last, :], wgo_rows[:, first:last, cols(c)])
-            return [part[:, t, :] for t in range(PACK)]
+        def load_wgo(c, tag):
+            part = ring.tile([P, PACK, HALF], F32, name="wgo_sb", tag=tag, bufs=1, align_bytes=64)
+            for q in (0, 2, 1, 3):
+                nc.sync.dma_start(part[32 * q : 32 * q + 32, :, :], wgo_rows[:, :, cols(c)])
+            return part
 
-        def load_x0(g, u):
-            pair = ring.tile([P, 2, S], F32, name="x0_pair", tag="raw", align_bytes=64)
+        def load_x0(g, u, tag):
+            pair = ring.tile([P, 2, S], F32, name="x0_pair", tag=tag, bufs=1, align_bytes=64)
             nc.sync.dma_start(pair[:], x0_rows[g][:, 2 * u : 2 * u + 2, :])
             return [pair[:, 0, :], pair[:, 1, :]]
 
@@ -118,13 +117,12 @@ def tile_list_tube_reading_correction_kernel(
         tab_w = []
         w1_raw = []
         for a in range(2):
-            tab_w.append(load_table(a))
-            w1_raw.append(load_rows(w1_rows[a], "raw", "w1_raw"))
+            tab_w.append(load_table(a, "AB"[a]))
+            w1_raw.append(load_rows(w1_rows[a], "CD"[a], "w1_raw"))
         place = keep.tile([P, S // 16], U16, name="place")
         nc.sync.dma_start(place[:], offs2)
 
-        ident = keep.tile([P, P], F32, name="ident")
-        make_identity(nc, ident[:])
+        ident = None
 
         v_s = keep.tile([P, S], U8, name="v_s", align_bytes=64)
         nc.vector.tensor_copy(v_s[:], tab_s[:].indirect(pick[:]))
@@ -141,24 +139,24 @@ def tile_list_tube_reading_correction_kernel(
                 joined[16 + 12 * q : 28 + 12 * q, :].bitcast(I32),
             )
 
+        v_w = [pick_words(tab_w[0], 0)]
+        tab_w.append(load_table(2, "A"))
         w4_c = keep.tile([P, PASSES * 2 * H], U8, name="w4_c", align_bytes=64)
         nc.vector.tensor_copy(
             w4_c[:].bitcast(U16).rearrange("p (a t m) -> p a t m", a=PASSES, t=PACK),
             w4_raw[:].bitcast(U16).rearrange("p (a m t) -> p a t m", a=PASSES, t=PACK),
         )
 
-        v_w = [pick_words(tab_w[0], 0)]
-        tab_w.append(load_table(2))
         w1_q = [quantize_weight(w1_raw[0], -1.0, "w1_0", 0)]
-        w1_raw.append(load_rows(w1_rows[2], "raw", "w1_raw"))
+        w1_raw.append(load_rows(w1_rows[2], "C", "w1_raw"))
         v_w.append(pick_words(tab_w[1], 1))
-        w3_raw = [load_rows(w3_rows[:, :, cols(0)], "wide", "w3_raw")]
+        w3_raw = [load_rows(w3_rows[:, :, cols(0)], "B", "w3_raw")]
         w1_q.append(quantize_weight(w1_raw[1], -1.0, "w1_1", 0))
-        spin_sb = [load_rows(spin_rows[:, :, cols(0)], "raw", "spin_sb")]
+        spin_sb = [load_rows(spin_rows[:, :, cols(0)], "D", "spin_sb")]
         v_w.append(pick_words(tab_w[2], 2))
-        wgo_sb = [load_wgo(0, [(0, 1), (1, PACK)])]
+        wgo_sb = [load_wgo(0, "A")]
         w1_q.append(quantize_weight(w1_raw[2], -1.0, "w1_2", VECTOR_SHARE))
-        spin_sb.append(load_rows(spin_rows[:, :, cols(1)], "raw", "spin_sb"))
+        spin_sb.append(load_rows(spin_rows[:, :, cols(1)], "C", "spin_sb"))
 
         def difference(c, blocks):
             width = HALF // blocks
@@ -199,7 +197,16 @@ def tile_list_tube_reading_correction_kernel(
         def hidden(c, sq, blocks):
             width = HALF // blocks
             h_bf = ring.tile([P, PACK * HALF], BF16, name="h_bf", tag="h_bf%d" % c, bufs=1, align_bytes=64)
-            for b in range(blocks):
+            if blocks == 1 and True:
+                sq4 = sq[:].rearrange("p (t j) -> p t j", t=PACK)
+                for b in range(2):
+                    js = slice(b * HALF // 2, (b + 1) * HALF // 2)
+                    nc.gpsimd.tensor_tensor(sq4[:, :, js], sq4[:, :, js], spin_sb[c][:, :, js], ALU.add)
+                    nc.scalar.copy(
+                        h_bf[:, PACK * js.start : PACK * js.stop].rearrange("p (c i t) -> p c t i", i=4, t=PACK),
+                        sq4[:, :, js].rearrange("p t (c i) -> p c t i", i=4),
+                    )
+            for b in range(blocks if blocks > 1 or not True else 0):
                 part = slice(PACK * b * width, PACK * (b + 1) * width)
                 nc.vector.tensor_tensor(
                     h_bf[:, part].rearrange("p (c i t) -> p c t i", i=4, t=PACK),
@@ -207,7 +214,7 @@ def tile_list_tube_reading_correction_kernel(
                     spin_sb[c][:, :, b * width : (b + 1) * width].rearrange("p t (c i) -> p c t i", i=4),
                     ALU.add,
                 )
-            h_c = keep.tile([P, HALF], U32, name="h_c%d" % c, align_bytes=64)
+            h_c = ring.tile([P, HALF], U32, name="h_c", tag="h_c%d" % c, bufs=1, align_bytes=64)
             h_s = keep.tile([P, HALF], U8, name="h_s%d" % c, align_bytes=64)
             nc.vector.quantize_mx(out=h_c[:].bitcast(FP8X4), scales=h_s[:], in_=h_bf[:])
             return h_c, h_s
@@ -232,17 +239,19 @@ def tile_list_tube_reading_correction_kernel(
                 start=True,
                 stop=True,
             )
-            if (i, c) == (0, 0):
-                nc.vector.scalar_tensor_tensor(corr(i, c), acc[:], sign(i), wgo_sb[c][t], ALU.mult, ALU.mult)
+            if (i, c) in [(0, 0), (6, 0), (6, 1), (7, 0), (7, 1)]:
+                nc.vector.scalar_tensor_tensor(corr(i, c), acc[:], sign(i), wgo_sb[c][:, t, :], ALU.mult, ALU.mult)
                 return
             nc.scalar.activation(corr(i, c), acc[:], ACT.Copy, scale=sign(i))
-            nc.gpsimd.tensor_tensor(corr(i, c), corr(i, c), wgo_sb[c][t], ALU.mult)
+            nc.gpsimd.tensor_tensor(corr(i, c), corr(i, c), wgo_sb[c][:, t, :], ALU.mult)
 
         def new_page(i):
-            if i == SLICES - 1:
+            if i == SLICES - 1 and True:
                 return ring.tile([P, PAGE_COLS], F32, name="page", tag="y_bf0", bufs=1, align_bytes=64)
             if i == EARLY - 1:
                 return ring.tile([P, PAGE_COLS], F32, name="page", tag="h_bf1", bufs=1, align_bytes=64)
+            if i == EARLY:
+                return ring.tile([P, PAGE_COLS], F32, name="page", tag="h_bf0", bufs=1, align_bytes=64)
             return ring.tile([P, PAGE_COLS], F32, name="page", tag="page", bufs=3)
 
         def scatter(i, c):
@@ -255,7 +264,10 @@ def tile_list_tube_reading_correction_kernel(
         def finish(i):
             g, t = divmod(i, PACK)
             page = pages[i]
-            gate = ring.tile([P, S], F32, name="gate", tag="gate", bufs=2)
+            if i == 0:
+                gate = ring.tile([P, S], F32, name="gate", tag="h_c1", bufs=1, align_bytes=64)
+            else:
+                gate = ring.tile([P, S], F32, name="gate", tag="gate", bufs=2)
             y = rows[:, (i + 0) * S : (i + 1) * S]
             if i == SLICES - 1:
                 dev = ring.tile([P, S], F32, name="dev", tag="sq", align_bytes=64)
@@ -267,9 +279,10 @@ def tile_list_tube_reading_correction_kernel(
                     nc.sync.dma_start(y_rows[g][:, t, cols(c)], y[:, cols(c)])
                 return
             nc.scalar.activation(gate[:], page[:, 0:S], ACT.Sigmoid, scale=sign(i))
+            dev = ring.tile([P, S], F32, name="dev", tag="dev", bufs=1)
             if i >= TURNED:
-                nc.gpsimd.tensor_tensor(y, page[:, 0:S], x0_sb[i], ALU.subtract)
-                nc.gpsimd.tensor_tensor(y, y, gate[:], ALU.mult)
+                nc.gpsimd.tensor_tensor(dev[:], page[:, 0:S], x0_sb[i], ALU.subtract)
+                (nc.vector if i in () else nc.gpsimd).tensor_tensor(y, dev[:], gate[:], ALU.mult)
                 nc.sync.dma_start(y_rows[g][:, t, :], y)
                 return
             turned = ring.tile([P, S], F32, name="turned", tag="sq", align_bytes=64)
@@ -289,8 +302,8 @@ def tile_list_tube_reading_correction_kernel(
                 for b in range(4):
                     blk = slice(c * HALF + b * P, c * HALF + (b + 1) * P)
                     nc.tensor.transpose(acc[:, b * P : (b + 1) * P], turned[:, blk], ident[:])
-                nc.scalar.copy(y[:, cols(c)], acc[:])
-            nc.gpsimd.tensor_tensor(y, y, gate[:], ALU.mult)
+                nc.scalar.copy(dev[:, cols(c)], acc[:])
+            nc.gpsimd.tensor_tensor(y, dev[:], gate[:], ALU.mult)
             nc.sync.dma_start(y_rows[g][:, t, :], y)
 
         def round_rows(y_bf, g, first, last, c, engine):
@@ -316,22 +329,21 @@ def tile_list_tube_reading_correction_kernel(
 
         pages = [new_page(i) for i in range(EARLY - 1)]
         w3_q = [quantize_weight(w3_raw[0], 1.0, "w3_0", W3_SHARE)]
-        wgo_sb.append(load_wgo(1, [(0, PACK)]))
+        w3_raw.append(load_rows(w3_rows[:, :, cols(1)], "B", "w3_raw"))
         h_q = [hidden(0, difference(0, PACK), PACK)]
-        w3_raw.append(load_rows(w3_rows[:, :, cols(1)], "raw", "w3_raw"))
+        wgo_sb.append(load_wgo(1, "D"))
         for i in range(EARLY - 1):
             correct(i, 0, i)
             scatter(i, 0)
-        h_q.append(hidden(1, difference(1, 1), 1))
+        sq = difference(1, 1)
+        w3_q.append(quantize_weight(w3_raw[1], 1.0, "w3_1", 0, "h_bf0", 1))
+        h_q.append(hidden(1, sq, 1))
         pages.append(new_page(EARLY - 1))
-        x0_sb = load_x0(0, 0)
         order = [(EARLY - 1, 0)] + [(i, 1) for i in range(EARLY)]
         order = order + [(i, c) for i in range(EARLY, SLICES) for c in range(HALVES)]
         for n, (i, c) in enumerate(order):
-            if (i, c) == (PACK, 0):
-                w3_q.append(quantize_weight(w3_raw[1], 1.0, "w3_1", 0, "h_bf0", 1))
-                x0_sb.extend(load_x0(0, 1))
             correct(i, c, (n + EARLY - 1) % PACK)
+        x0_sb = load_x0(0, 0, "B") + load_x0(0, 1, "C") + load_x0(1, 0, "A") + load_x0(1, 1, "D")
         for i, c in order[: EARLY + 1]:
             scatter(i, c)
         y_bf = [ring.tile([P, PACK * S], BF16, name="y_bf", tag="y_bf%d" % g, bufs=1, align_bytes=64) for g in range(GROUPS)]
@@ -342,8 +354,6 @@ def tile_list_tube_reading_correction_kernel(
                 pages.append(new_page(i + 1))
                 scatter_whole(i + 1)
             finish(i)
-            if i in (1, 3):
-                x0_sb.extend(load_x0(1, i // 2))
             if i == PACK:
                 for k in range(4):
                     round_rows(y_bf[0], 0, 0, PACK, slice(k * S // 4, (k + 1) * S // 4), nc.scalar.copy)

@@ -1,7 +1,6 @@
 from contextlib import ExitStack
 
 import concourse.mybir as mybir
-from concourse.masks import make_identity
 
 K, T, S, H, N = 1536, 2048, 1024, 512, 1024
 FLOPS = 2 * (2 * K * H * S + H * N * S)
@@ -22,16 +21,18 @@ PACK = 4
 K_PASS = P * PACK
 PASSES = K // K_PASS
 GROUPS = N // K_PASS
-HALF = 512
-HALVES = S // HALF
-LIST_COLS = HALF // 16
-QUADS = 4
-PAGE_COLS = 1408
 SLICES = GROUPS * PACK
+QUADS = 4
+HALF = 512
+QUARTER = HALF // 2
+HALVES = S // HALF
+PER_COL = 16
+RUN = 4
+STACK = 16
+PAGE_COLS = 1408
 EARLY = 4
-TURNED = 0
-VECTOR_SHARE = 72
-W3_SHARE = 128
+ON_VECTOR = 3
+W1_ON_VECTOR = 56
 
 
 def tile_list_tube_reading_correction_kernel(
@@ -40,13 +41,13 @@ def tile_list_tube_reading_correction_kernel(
     nc = tc.nc
     with ExitStack() as ctx:
         keep = ctx.enter_context(tc.tile_pool(name="keep", bufs=1))
-        ring = ctx.enter_context(tc.tile_pool(name="ring", bufs=2))
+        reuse = ctx.enter_context(tc.tile_pool(name="reuse", bufs=1))
         psum = ctx.enter_context(tc.psum_pool(name="psum", bufs=1))
 
         def bank(k):
             return psum.tile([P, HALF], F32, name="bank%d" % k, tag="bank%d" % k)
 
-        def cols(c):
+        def half(c):
             return slice(c * HALF, (c + 1) * HALF)
 
         w1_rows = w1.rearrange("(a p j) r -> a p j r", p=P, j=PACK)
@@ -56,42 +57,44 @@ def tile_list_tube_reading_correction_kernel(
         y_rows = out_0.rearrange("(g p t) m -> g p t m", p=P, t=PACK)
         wgo_rows = wgo.rearrange("(m t) j -> m t j", t=PACK)
 
+
         def load_scale_rows(scales, width, name):
             stacked = keep.tile([P, width], U8, name=name, align_bytes=64)
-            nc.sync.dma_start(stacked[16:64, :].bitcast(I32), scales.bitcast(I32).rearrange("a q t -> q a t"))
-            nc.vector.memset(stacked[0:16, :].bitcast(I32), 0)
+            nc.sync.dma_start(stacked[STACK:64, :].bitcast(I32), scales.bitcast(I32).rearrange("a q t -> q a t"))
+            nc.vector.memset(stacked[0:STACK, :].bitcast(I32), 0)
             nc.vector.memset(stacked[64:P, :].bitcast(I32), 0)
             return stacked
 
         def load_table(a, tag):
-            words = ring.tile([P, T], U32, name="tab_w", tag=tag, bufs=1, align_bytes=64)
+            words = reuse.tile([P, T], U32, name="tab_w", tag=tag, align_bytes=64)
             nc.sync.dma_start(words[:].bitcast(I32), tab_words[a].rearrange("p t i -> p (t i)").bitcast(I32))
             return words
 
-        def load_rows(rows, tag, name):
-            raw = ring.tile([P, PACK, HALF], F32, name=name, tag=tag, bufs=1, align_bytes=64)
-            nc.sync.dma_start(raw[:], rows)
+        def load_rows(source, name, tag):
+            raw = reuse.tile([P, PACK, HALF], F32, name=name, tag=tag, align_bytes=64)
+            nc.sync.dma_start(raw[:], source)
             return raw
 
-        def load_wgo(c, tag):
-            part = ring.tile([P, PACK, HALF], F32, name="wgo_sb", tag=tag, bufs=1, align_bytes=64)
-            for q in (0, 2, 1, 3):
-                nc.sync.dma_start(part[32 * q : 32 * q + 32, :, :], wgo_rows[:, :, cols(c)])
+        def load_wgo(c, tag, row_sets):
+            part = reuse.tile([P, PACK, HALF], F32, name="wgo_sb", tag=tag, align_bytes=64)
+            for ts in row_sets:
+                for q in (0, 2, 1, 3):
+                    nc.sync.dma_start(part[32 * q : 32 * q + 32, ts, :], wgo_rows[:, ts, half(c)])
             return part
 
         def load_x0(g, u, tag):
-            pair = ring.tile([P, 2, S], F32, name="x0_pair", tag=tag, bufs=1, align_bytes=64)
+            pair = reuse.tile([P, 2, S], F32, name="x0_pair", tag=tag, align_bytes=64)
             nc.sync.dma_start(pair[:], x0_rows[g][:, 2 * u : 2 * u + 2, :])
             return [pair[:, 0, :], pair[:, 1, :]]
 
-        def quantize_weight(raw, sign, name, shared, tag="bf", bufs=2):
-            dealt = ring.tile([P, PACK * HALF], BF16, name="dealt", tag=tag, bufs=bufs, align_bytes=64)
-            dst = dealt[:].rearrange("p (t m j) -> p m j t", t=PACK, j=PACK)
-            src = raw[:].rearrange("p j (m t) -> p m j t", t=PACK)
-            if shared < P:
-                nc.scalar.activation(dst[:, shared:, :, :], src[:, shared:, :, :], ACT.Copy, scale=sign)
-            if shared:
-                nc.vector.tensor_scalar(dst[:, :shared, :, :], src[:, :shared, :, :], sign, None, ALU.mult)
+        def quantize_weight(raw, sign, name, on_vector, tag, bufs):
+            dealt = reuse.tile([P, PACK * HALF], BF16, name="dealt", tag=tag, bufs=bufs, align_bytes=64)
+            dst = dealt[:].rearrange("p (t m j) -> p m t j", t=PACK, j=PACK)
+            src = raw[:].rearrange("p j (m t) -> p m t j", t=PACK)
+            if on_vector < P:
+                nc.scalar.activation(dst[:, on_vector:, :, :], src[:, on_vector:, :, :], ACT.Copy, scale=sign)
+            if on_vector > 0:
+                nc.vector.tensor_scalar(dst[:, :on_vector, :, :], src[:, :on_vector, :, :], sign, None, ALU.mult)
             codes = keep.tile([P, HALF], U32, name=name + "_codes", align_bytes=64)
             scales = keep.tile([P, HALF], U8, name=name + "_scales", align_bytes=64)
             nc.vector.quantize_mx(out=codes[:].bitcast(FP8X4), scales=scales[:], in_=dealt[:])
@@ -101,11 +104,12 @@ def tile_list_tube_reading_correction_kernel(
             picked = []
             for c in range(HALVES):
                 part = keep.tile([P, HALF], U32, name="v_w%d_%d" % (a, c), align_bytes=64)
-                nc.vector.tensor_copy(part[:], words[:].indirect(pick[:, c * LIST_COLS : (c + 1) * LIST_COLS]))
+                entries = pick[:, c * HALF // PER_COL : (c + 1) * HALF // PER_COL]
+                nc.vector.tensor_copy(part[:], words[:].indirect(entries))
                 picked.append(part)
             return picked
 
-        pick = keep.tile([P, S // 16], U16, name="pick")
+        pick = keep.tile([P, S // PER_COL], U16, name="pick")
         nc.sync.dma_start(pick[:], offs)
         tab_s = load_scale_rows(tab_scales, T, "tab_s")
         w4_s_raw = load_scale_rows(w4_scales, H, "w4_s_raw")
@@ -114,15 +118,12 @@ def tile_list_tube_reading_correction_kernel(
             w4_raw[:].bitcast(I32).rearrange("p (a c) -> p a c", a=PASSES),
             w4_words.bitcast(I32).rearrange("a p c -> p a c"),
         )
-        tab_w = []
-        w1_raw = []
-        for a in range(2):
-            tab_w.append(load_table(a, "AB"[a]))
-            w1_raw.append(load_rows(w1_rows[a], "CD"[a], "w1_raw"))
-        place = keep.tile([P, S // 16], U16, name="place")
+        tab_w = [load_table(0, "load0")]
+        w1_raw = [load_rows(w1_rows[0], "w1_raw", "load2")]
+        tab_w.append(load_table(1, "load1"))
+        w1_raw.append(load_rows(w1_rows[1], "w1_raw", "load3"))
+        place = keep.tile([P, S // PER_COL], U16, name="place")
         nc.sync.dma_start(place[:], offs2)
-
-        ident = None
 
         v_s = keep.tile([P, S], U8, name="v_s", align_bytes=64)
         nc.vector.tensor_copy(v_s[:], tab_s[:].indirect(pick[:]))
@@ -133,233 +134,217 @@ def tile_list_tube_reading_correction_kernel(
         )
         nc.vector.tensor_copy(joined[:, 0:S].bitcast(I32), v_s[:].bitcast(I32))
         given_s = keep.tile([P, PASSES * (S + H)], U8, name="given_s", align_bytes=64)
+        per_quad = 4 * PASSES
         for q in range(QUADS):
             nc.scalar.dma_start(
                 given_s[32 * q : 32 * q + 4, :].bitcast(I32).rearrange("r (a t) -> r a t", a=PASSES),
-                joined[16 + 12 * q : 28 + 12 * q, :].bitcast(I32),
+                joined[STACK + per_quad * q : STACK + per_quad * (q + 1), :].bitcast(I32),
             )
 
-        v_w = [pick_words(tab_w[0], 0)]
-        tab_w.append(load_table(2, "A"))
         w4_c = keep.tile([P, PASSES * 2 * H], U8, name="w4_c", align_bytes=64)
         nc.vector.tensor_copy(
             w4_c[:].bitcast(U16).rearrange("p (a t m) -> p a t m", a=PASSES, t=PACK),
             w4_raw[:].bitcast(U16).rearrange("p (a m t) -> p a t m", a=PASSES, t=PACK),
         )
 
-        w1_q = [quantize_weight(w1_raw[0], -1.0, "w1_0", 0)]
-        w1_raw.append(load_rows(w1_rows[2], "C", "w1_raw"))
+        v_w = [pick_words(tab_w[0], 0)]
+        tab_w.append(load_table(2, "load0"))
+        w1_q = [quantize_weight(w1_raw[0], -1.0, "w1_0", 0, "dealt", 2)]
+        w1_raw.append(load_rows(w1_rows[2], "w1_raw", "load2"))
         v_w.append(pick_words(tab_w[1], 1))
-        w3_raw = [load_rows(w3_rows[:, :, cols(0)], "B", "w3_raw")]
-        w1_q.append(quantize_weight(w1_raw[1], -1.0, "w1_1", 0))
-        spin_sb = [load_rows(spin_rows[:, :, cols(0)], "D", "spin_sb")]
+        w3_raw = [load_rows(w3_rows[:, :, half(0)], "w3_raw", "load1")]
+        w1_q.append(quantize_weight(w1_raw[1], -1.0, "w1_1", 0, "dealt", 2))
+        spin_sb = [load_rows(spin_rows[:, :, half(0)], "spin_sb", "load3")]
         v_w.append(pick_words(tab_w[2], 2))
-        wgo_sb = [load_wgo(0, "A")]
-        w1_q.append(quantize_weight(w1_raw[2], -1.0, "w1_2", VECTOR_SHARE))
-        spin_sb.append(load_rows(spin_rows[:, :, cols(1)], "C", "spin_sb"))
+        wgo_sb = [load_wgo(0, "load0", [slice(0, 1), slice(1, PACK)])]
+        w1_q.append(quantize_weight(w1_raw[2], -1.0, "w1_2", W1_ON_VECTOR, "dealt", 2))
+        spin_sb.append(load_rows(spin_rows[:, :, half(1)], "spin_sb", "load2"))
 
-        def difference(c, blocks):
-            width = HALF // blocks
-            d_bank = [bank(PACK * c + k) for k in range(PACK)]
 
-            def target(t, b):
-                if blocks == 1:
-                    return d_bank[t][:]
-                return d_bank[b][:, t * P : (t + 1) * P]
-
-            for a in range(PASSES):
+        def squared_difference(c):
+            d_bank = [bank(b) for b in range(PACK)]
+            steps = [("w4", 0)]
+            for a in range(1, PASSES):
+                steps.extend([("w4", a), ("w1", a - 1)])
+            steps.append(("w1", PASSES - 1))
+            for n, (weight, a) in enumerate(steps):
                 base = a * (S + H)
-                for own in (False, True):
-                    for b in range(blocks):
-                        moving = v_w[a][c][:, b * width : (b + 1) * width].bitcast(FP8X4)
-                        first = base + c * HALF + b * width
-                        for t in range(PACK):
-                            if own:
-                                held = w1_q[a][0][:, t * P : (t + 1) * P].bitcast(FP8X4)
-                                held_s = w1_q[a][1][:, t * P : (t + 1) * P]
-                            else:
-                                held = w4_c[:, 2 * (a * H + t * P) : 2 * (a * H + (t + 1) * P)].bitcast(FP4X4)
-                                held_s = given_s[:, base + S + t * P : base + S + (t + 1) * P]
-                            nc.tensor.matmul_mx(
-                                out=target(t, b),
-                                lhsT=held,
-                                lhsT_scale=held_s,
-                                rhs=moving,
-                                rhs_scale=given_s[:, first : first + width],
-                                start=(a == 0 and not own and (blocks == 1 or t == 0)),
-                                stop=(a == PASSES - 1 and own and (blocks == 1 or t == PACK - 1)),
-                            )
-            sq = ring.tile([P, PACK * HALF], F32, name="sq", tag="sq", align_bytes=64)
-            for k in range(PACK):
-                nc.scalar.activation(sq[:, k * HALF : (k + 1) * HALF], d_bank[k][:], ACT.Square)
-            return sq
+                for b in range(PACK):
+                    first = base + c * HALF + b * P
+                    for t in range(PACK):
+                        if weight == "w1":
+                            held = w1_q[a][0][:, t * P : (t + 1) * P].bitcast(FP8X4)
+                            held_s = w1_q[a][1][:, t * P : (t + 1) * P]
+                        else:
+                            held = w4_c[:, 2 * (a * H + t * P) : 2 * (a * H + (t + 1) * P)].bitcast(FP4X4)
+                            held_s = given_s[:, base + S + t * P : base + S + (t + 1) * P]
+                        nc.tensor.matmul_mx(
+                            out=d_bank[b][:, t * P : (t + 1) * P],
+                            lhsT=held,
+                            lhsT_scale=held_s,
+                            rhs=v_w[a][c][:, b * P : (b + 1) * P].bitcast(FP8X4),
+                            rhs_scale=given_s[:, first : first + P],
+                            start=(n == 0 and t == 0),
+                            stop=(n == len(steps) - 1 and t == PACK - 1),
+                        )
+            sq = reuse.tile([P, PACK, HALF], F32, name="sq", tag="sq%d" % c, align_bytes=64)
+            for b in range(PACK):
+                nc.scalar.activation(sq[:, b, :], d_bank[b][:], ACT.Square)
+            return [sq[:, b, :].rearrange("p (t j) -> p t j", t=PACK) for b in range(PACK)]
 
-        def hidden(c, sq, blocks):
-            width = HALF // blocks
-            h_bf = ring.tile([P, PACK * HALF], BF16, name="h_bf", tag="h_bf%d" % c, bufs=1, align_bytes=64)
-            if blocks == 1 and True:
-                sq4 = sq[:].rearrange("p (t j) -> p t j", t=PACK)
-                for b in range(2):
-                    js = slice(b * HALF // 2, (b + 1) * HALF // 2)
-                    nc.gpsimd.tensor_tensor(sq4[:, :, js], sq4[:, :, js], spin_sb[c][:, :, js], ALU.add)
-                    nc.scalar.copy(
-                        h_bf[:, PACK * js.start : PACK * js.stop].rearrange("p (c i t) -> p c t i", i=4, t=PACK),
-                        sq4[:, :, js].rearrange("p t (c i) -> p c t i", i=4),
-                    )
-            for b in range(blocks if blocks > 1 or not True else 0):
-                part = slice(PACK * b * width, PACK * (b + 1) * width)
+        def interleaved(tile, first, width):
+            return tile[:, PACK * first : PACK * (first + width)].rearrange("p (c i t) -> p c t i", i=RUN, t=PACK)
+
+        def in_runs(rows4):
+            return rows4.rearrange("p t (c i) -> p c t i", i=RUN)
+
+        def h_tiles(c):
+            h_bf = reuse.tile([P, PACK * HALF], BF16, name="h_bf", tag="h_bf%d" % c, align_bytes=64)
+            h_c = reuse.tile([P, HALF], U32, name="h_c", tag="h_c%d" % c, align_bytes=64)
+            h_s = keep.tile([P, HALF], U8, name="h_s%d" % c, align_bytes=64)
+            return h_bf, h_c, h_s
+
+        def quantize_columns(codes, scales, values, first, width):
+            nc.vector.quantize_mx(
+                out=codes[:, first : first + width].bitcast(FP8X4),
+                scales=scales[:, first : first + width],
+                in_=values[:, PACK * first : PACK * (first + width)],
+            )
+
+        def first_half_of_h(sq):
+            h_bf, h_c, h_s = h_tiles(0)
+            for b in range(PACK):
                 nc.vector.tensor_tensor(
-                    h_bf[:, part].rearrange("p (c i t) -> p c t i", i=4, t=PACK),
-                    sq[:, part].rearrange("p (t c i) -> p c t i", i=4, t=PACK),
-                    spin_sb[c][:, :, b * width : (b + 1) * width].rearrange("p t (c i) -> p c t i", i=4),
+                    interleaved(h_bf, b * P, P),
+                    in_runs(sq[b]),
+                    in_runs(spin_sb[0][:, :, b * P : (b + 1) * P]),
                     ALU.add,
                 )
-            h_c = ring.tile([P, HALF], U32, name="h_c", tag="h_c%d" % c, bufs=1, align_bytes=64)
-            h_s = keep.tile([P, HALF], U8, name="h_s%d" % c, align_bytes=64)
-            nc.vector.quantize_mx(out=h_c[:].bitcast(FP8X4), scales=h_s[:], in_=h_bf[:])
+                if (b + 1) * P % QUARTER == 0:
+                    quantize_columns(h_c, h_s, h_bf, (b + 1) * P - QUARTER, QUARTER)
             return h_c, h_s
 
-        rows = keep.tile([P, (SLICES + 0) * S], F32, name="rows")
+        def second_half_of_h(sq):
+            h_bf, h_c, h_s = h_tiles(1)
+            for b in range(PACK):
+                nc.gpsimd.tensor_tensor(sq[b], sq[b], spin_sb[1][:, :, b * P : (b + 1) * P], ALU.add)
+                nc.scalar.copy(interleaved(h_bf, b * P, P), in_runs(sq[b]))
+            quantize_columns(h_c, h_s, h_bf, 0, HALF)
+            return h_c, h_s
 
-        def corr(i, c):
-            return rows[:, i * S + c * HALF : i * S + (c + 1) * HALF]
+        rows = keep.tile([P, SLICES, S], F32, name="rows")
 
-        def sign(i):
-            return -1.0 if i < TURNED else 1.0
+        def staged(i, first, width):
+            if (i, first) == (0, HALF):
+                return held_back[:]
+            return rows[:, i, first : first + width]
 
-        def correct(i, c, k):
+        def weighted_product(i, first, width, k, on_vector):
             g, t = divmod(i, PACK)
+            c, inside = divmod(first, HALF)
             acc = bank(k)
             nc.tensor.matmul_mx(
-                out=acc[:],
+                out=acc[:, 0:width],
                 lhsT=w3_q[g][0][:, t * P : (t + 1) * P].bitcast(FP8X4),
                 lhsT_scale=w3_q[g][1][:, t * P : (t + 1) * P],
-                rhs=h_q[c][0][:].bitcast(FP8X4),
-                rhs_scale=h_q[c][1][:],
+                rhs=h_q[c][0][:, inside : inside + width].bitcast(FP8X4),
+                rhs_scale=h_q[c][1][:, inside : inside + width],
                 start=True,
                 stop=True,
             )
-            if (i, c) in [(0, 0), (6, 0), (6, 1), (7, 0), (7, 1)]:
-                nc.vector.scalar_tensor_tensor(corr(i, c), acc[:], sign(i), wgo_sb[c][:, t, :], ALU.mult, ALU.mult)
-                return
-            nc.scalar.activation(corr(i, c), acc[:], ACT.Copy, scale=sign(i))
-            nc.gpsimd.tensor_tensor(corr(i, c), corr(i, c), wgo_sb[c][:, t, :], ALU.mult)
+            values = staged(i, first, width)
+            factor = wgo_sb[c][:, t, inside : inside + width]
+            if on_vector:
+                nc.vector.tensor_tensor(values, acc[:, 0:width], factor, ALU.mult)
+            else:
+                nc.scalar.copy(values, acc[:, 0:width])
+                nc.gpsimd.tensor_tensor(values, values, factor, ALU.mult)
 
         def new_page(i):
-            if i == SLICES - 1 and True:
-                return ring.tile([P, PAGE_COLS], F32, name="page", tag="y_bf0", bufs=1, align_bytes=64)
-            if i == EARLY - 1:
-                return ring.tile([P, PAGE_COLS], F32, name="page", tag="h_bf1", bufs=1, align_bytes=64)
-            if i == EARLY:
-                return ring.tile([P, PAGE_COLS], F32, name="page", tag="h_bf0", bufs=1, align_bytes=64)
-            return ring.tile([P, PAGE_COLS], F32, name="page", tag="page", bufs=3)
+            if i == SLICES - 1:
+                return reuse.tile([P, PAGE_COLS], F32, name="page", tag="y_bf0", align_bytes=64)
+            return reuse.tile([P, PAGE_COLS], F32, name="page", tag="page", bufs=EARLY + 1)
 
-        def scatter(i, c):
-            window = pages[i][:].indirect(place[:, c * LIST_COLS : (c + 1) * LIST_COLS])
-            nc.vector.tensor_copy(window, corr(i, c))
-
-        def scatter_whole(i):
-            nc.vector.tensor_copy(pages[i][:].indirect(place[:]), rows[:, i * S : (i + 1) * S])
+        def scatter(i, first, width):
+            entries = place[:, first // PER_COL : (first + width) // PER_COL]
+            nc.vector.tensor_copy(pages[i][:].indirect(entries), staged(i, first, width))
 
         def finish(i):
             g, t = divmod(i, PACK)
-            page = pages[i]
+            page = pages[i][:, 0:S]
             if i == 0:
-                gate = ring.tile([P, S], F32, name="gate", tag="h_c1", bufs=1, align_bytes=64)
+                gate = reuse.tile([P, S], F32, name="gate", tag="h_c1", align_bytes=64)
             else:
-                gate = ring.tile([P, S], F32, name="gate", tag="gate", bufs=2)
-            y = rows[:, (i + 0) * S : (i + 1) * S]
-            if i == SLICES - 1:
-                dev = ring.tile([P, S], F32, name="dev", tag="sq", align_bytes=64)
-                for c in range(HALVES):
-                    nc.scalar.activation(gate[:, cols(c)], page[:, cols(c)], ACT.Sigmoid)
-                    nc.vector.tensor_tensor(dev[:, cols(c)], page[:, cols(c)], x0_sb[i][:, cols(c)], ALU.subtract)
-                for c in range(HALVES):
-                    nc.vector.tensor_tensor(y[:, cols(c)], dev[:, cols(c)], gate[:, cols(c)], ALU.mult)
-                    nc.sync.dma_start(y_rows[g][:, t, cols(c)], y[:, cols(c)])
-                return
-            nc.scalar.activation(gate[:], page[:, 0:S], ACT.Sigmoid, scale=sign(i))
-            dev = ring.tile([P, S], F32, name="dev", tag="dev", bufs=1)
-            if i >= TURNED:
-                nc.gpsimd.tensor_tensor(dev[:], page[:, 0:S], x0_sb[i], ALU.subtract)
-                (nc.vector if i in () else nc.gpsimd).tensor_tensor(y, dev[:], gate[:], ALU.mult)
+                gate = reuse.tile([P, S], F32, name="gate", tag="gate", bufs=2)
+            dev = reuse.tile([P, S], F32, name="dev", tag="dev", bufs=2)
+            y = rows[:, i, :]
+            if i < SLICES - 1:
+                nc.scalar.activation(gate[:], page, ACT.Sigmoid)
+                nc.gpsimd.tensor_tensor(dev[:], page, x0_sb[i], ALU.subtract)
+                nc.gpsimd.tensor_tensor(y, dev[:], gate[:], ALU.mult)
                 nc.sync.dma_start(y_rows[g][:, t, :], y)
                 return
-            turned = ring.tile([P, S], F32, name="turned", tag="sq", align_bytes=64)
             for c in range(HALVES):
-                acc = bank(4 + c)
-                for b in range(4):
-                    blk = slice(c * HALF + b * P, c * HALF + (b + 1) * P)
-                    nc.tensor.matmul(
-                        acc[:, b * P : (b + 1) * P], x0_sb[i][:, blk], ident[:], start=True, stop=False, is_transpose=True
-                    )
-                    nc.tensor.matmul(
-                        acc[:, b * P : (b + 1) * P], page[:, blk], ident[:], start=False, stop=True, is_transpose=True
-                    )
-                nc.scalar.activation(turned[:, cols(c)], acc[:], ACT.Copy, scale=-1.0)
+                nc.scalar.activation(gate[:, half(c)], page[:, half(c)], ACT.Sigmoid)
+                nc.vector.tensor_tensor(dev[:, half(c)], page[:, half(c)], x0_sb[i][:, half(c)], ALU.subtract)
             for c in range(HALVES):
-                acc = bank(6 + c)
-                for b in range(4):
-                    blk = slice(c * HALF + b * P, c * HALF + (b + 1) * P)
-                    nc.tensor.transpose(acc[:, b * P : (b + 1) * P], turned[:, blk], ident[:])
-                nc.scalar.copy(dev[:, cols(c)], acc[:])
-            nc.gpsimd.tensor_tensor(y, dev[:], gate[:], ALU.mult)
-            nc.sync.dma_start(y_rows[g][:, t, :], y)
+                nc.vector.tensor_tensor(y[:, half(c)], dev[:, half(c)], gate[:, half(c)], ALU.mult)
+                nc.sync.dma_start(y_rows[g][:, t, half(c)], y[:, half(c)])
 
-        def round_rows(y_bf, g, first, last, c, engine):
-            y4 = rows[:, PACK * g * S : PACK * (g + 1) * S].rearrange("p (t m) -> p t m", t=PACK)
-            dst = y_bf[:, PACK * c.start : PACK * c.stop].rearrange("p (c i t) -> p c t i", i=4, t=PACK)
-            src = y4[:, :, c].rearrange("p t (c i) -> p c t i", i=4)
-            engine(dst[:, :, first:last, :], src[:, :, first:last, :])
+        def round_rows(g, ts, first, width, copy):
+            src = in_runs(rows[:, PACK * g : PACK * (g + 1), first : first + width])
+            copy(interleaved(y_bf[g], first, width)[:, :, ts, :], src[:, :, ts, :])
 
-        def planes(y_bf, g):
+        def planes(g):
             y_c = keep.tile([P, S], U32, name="y_c%d" % g, align_bytes=64)
             y_s = keep.tile([P, S], U8, name="y_s%d" % g, align_bytes=64)
             words_out = out_1[g].rearrange("p m t -> p (m t)").bitcast(I32)
-            for c in (1, 0):
-                nc.vector.quantize_mx(
-                    out=y_c[:, cols(c)].bitcast(FP8X4),
-                    scales=y_s[:, cols(c)],
-                    in_=y_bf[:, PACK * c * HALF : PACK * (c + 1) * HALF],
-                )
-                nc.sync.dma_start(words_out[:, cols(c)], y_c[:, cols(c)].bitcast(I32))
+            for c in reversed(range(HALVES)):
+                quantize_columns(y_c, y_s, y_bf[g], c * HALF, HALF)
+                nc.sync.dma_start(words_out[:, half(c)], y_c[:, half(c)].bitcast(I32))
             for q in range(QUADS):
-                eng = nc.scalar if g == GROUPS - 1 and q % 2 == 1 else nc.sync
-                eng.dma_start(out_2[g, 4 * q : 4 * q + 4, :].bitcast(I32), y_s[32 * q : 32 * q + 4, :].bitcast(I32))
+                queue = nc.scalar if g == GROUPS - 1 and q % 2 == 1 else nc.sync
+                queue.dma_start(out_2[g, 4 * q : 4 * q + 4, :].bitcast(I32), y_s[32 * q : 32 * q + 4, :].bitcast(I32))
 
-        pages = [new_page(i) for i in range(EARLY - 1)]
-        w3_q = [quantize_weight(w3_raw[0], 1.0, "w3_0", W3_SHARE)]
-        w3_raw.append(load_rows(w3_rows[:, :, cols(1)], "B", "w3_raw"))
-        h_q = [hidden(0, difference(0, PACK), PACK)]
-        wgo_sb.append(load_wgo(1, "D"))
-        for i in range(EARLY - 1):
-            correct(i, 0, i)
-            scatter(i, 0)
-        sq = difference(1, 1)
-        w3_q.append(quantize_weight(w3_raw[1], 1.0, "w3_1", 0, "h_bf0", 1))
-        h_q.append(hidden(1, sq, 1))
-        pages.append(new_page(EARLY - 1))
-        order = [(EARLY - 1, 0)] + [(i, 1) for i in range(EARLY)]
-        order = order + [(i, c) for i in range(EARLY, SLICES) for c in range(HALVES)]
-        for n, (i, c) in enumerate(order):
-            correct(i, c, (n + EARLY - 1) % PACK)
-        x0_sb = load_x0(0, 0, "B") + load_x0(0, 1, "C") + load_x0(1, 0, "A") + load_x0(1, 1, "D")
-        for i, c in order[: EARLY + 1]:
-            scatter(i, c)
-        y_bf = [ring.tile([P, PACK * S], BF16, name="y_bf", tag="y_bf%d" % g, bufs=1, align_bytes=64) for g in range(GROUPS)]
+        pages = [new_page(i) for i in range(EARLY)]
+        w3_q = [quantize_weight(w3_raw[0], 1.0, "w3_0", P, "dealt", 2)]
+        w3_raw.append(load_rows(w3_rows[:, :, half(1)], "w3_raw", "load1"))
+        h_q = [first_half_of_h(squared_difference(0))]
+        wgo_sb.append(load_wgo(1, "load3", [slice(0, PACK)]))
+
+        opening = [(0, 0, QUARTER), (0, QUARTER, QUARTER)] + [(i, 0, HALF) for i in range(1, EARLY)]
+        for n, (i, first, width) in enumerate(opening):
+            weighted_product(i, first, width, PACK + n % PACK, i == 0)
+            scatter(i, first, width)
+
+        h_q.append(second_half_of_h(squared_difference(1)))
+        w3_q.append(quantize_weight(w3_raw[1], 1.0, "w3_1", 0, "sq1", 1))
+        held_back = reuse.tile([P, HALF], F32, name="held_back", tag="sq1", align_bytes=64)
+        later = [(i, 1) for i in range(EARLY)] + [(i, c) for i in range(EARLY, SLICES) for c in range(HALVES)]
+        for n, (i, c) in enumerate(later):
+            on_vector = i == 0 or i >= SLICES - ON_VECTOR
+            weighted_product(i, c * HALF, HALF, n % (2 * PACK), on_vector)
+        x0_sb = load_x0(0, 0, "load1") + load_x0(0, 1, "load2") + load_x0(1, 0, "load0") + load_x0(1, 1, "load3")
+        for i in range(EARLY):
+            scatter(i, HALF, HALF)
+
+        y_bf = [
+            reuse.tile([P, PACK * S], BF16, name="y_bf", tag="y_bf%d" % g, align_bytes=64) for g in range(GROUPS)
+        ]
         for i in range(SLICES):
-            if i == SLICES - 2:
-                planes(y_bf[0], 0)
-            if EARLY <= i + 1 < SLICES:
-                pages.append(new_page(i + 1))
-                scatter_whole(i + 1)
+            following = i + 1
+            if following == SLICES - 1:
+                planes(0)
+            if EARLY <= following < SLICES:
+                pages.append(new_page(following))
+                scatter(following, 0, S)
             finish(i)
             if i == PACK:
-                for k in range(4):
-                    round_rows(y_bf[0], 0, 0, PACK, slice(k * S // 4, (k + 1) * S // 4), nc.scalar.copy)
+                for first in range(0, S, QUARTER):
+                    round_rows(0, slice(0, PACK), first, QUARTER, nc.scalar.copy)
             if i == SLICES - 2:
                 for c in range(HALVES):
-                    round_rows(y_bf[1], 1, 0, 2, cols(c), nc.scalar.copy)
-        round_rows(y_bf[1], 1, 2, 4, cols(0), nc.scalar.copy)
-        round_rows(y_bf[1], 1, 2, 4, cols(1), nc.vector.tensor_copy)
-        planes(y_bf[1], 1)
+                    round_rows(1, slice(0, 2), c * HALF, HALF, nc.scalar.copy)
+        round_rows(1, slice(2, PACK), 0, HALF, nc.scalar.copy)
+        round_rows(1, slice(2, PACK), HALF, HALF, nc.vector.tensor_copy)
+        planes(1)

from contextlib import ExitStack

import concourse.mybir as mybir

K, T, S, H, N = 1536, 2048, 1024, 512, 1024
FLOPS = 2 * (2 * K * H * S + H * N * S)

F32 = mybir.dt.float32
BF16 = mybir.dt.bfloat16
I32 = mybir.dt.int32
U32 = mybir.dt.uint32
U16 = mybir.dt.uint16
U8 = mybir.dt.uint8
FP8X4 = mybir.dt.float8_e4m3fn_x4
FP4X4 = mybir.dt.float4_e2m1fn_x4
ACT = mybir.ActivationFunctionType
ALU = mybir.AluOpType

P = 128
PACK = 4
K_PASS = P * PACK
PASSES = K // K_PASS
GROUPS = N // K_PASS
SLICES = GROUPS * PACK
QUADS = 4
HALF = 512
QUARTER = HALF // 2
HALVES = S // HALF
PER_COL = 16
RUN = 4
STACK = 16
PAGE_COLS = 1408
EARLY = 4
ON_VECTOR = 3
W1_ON_VECTOR = 56


def tile_list_tube_reading_correction_kernel(
    tc, tab_words, tab_scales, offs, w1, w4_words, w4_scales, spin, w3, offs2, wgo, x0, out_0, out_1, out_2
):
    nc = tc.nc
    with ExitStack() as ctx:
        keep = ctx.enter_context(tc.tile_pool(name="keep", bufs=1))
        reuse = ctx.enter_context(tc.tile_pool(name="reuse", bufs=1))
        psum = ctx.enter_context(tc.psum_pool(name="psum", bufs=1))

        def bank(k):
            return psum.tile([P, HALF], F32, name="bank%d" % k, tag="bank%d" % k)

        def half(c):
            return slice(c * HALF, (c + 1) * HALF)

        w1_rows = w1.rearrange("(a p j) r -> a p j r", p=P, j=PACK)
        w3_rows = w3.rearrange("(p j) n -> p j n", j=PACK)
        spin_rows = spin.rearrange("(p t) j -> p t j", t=PACK)
        x0_rows = x0.rearrange("(g p t) m -> g p t m", p=P, t=PACK)
        y_rows = out_0.rearrange("(g p t) m -> g p t m", p=P, t=PACK)
        wgo_rows = wgo.rearrange("(m t) j -> m t j", t=PACK)


        def load_scale_rows(scales, width, name):
            stacked = keep.tile([P, width], U8, name=name, align_bytes=64)
            nc.sync.dma_start(stacked[STACK:64, :].bitcast(I32), scales.bitcast(I32).rearrange("a q t -> q a t"))
            nc.vector.memset(stacked[0:STACK, :].bitcast(I32), 0)
            nc.vector.memset(stacked[64:P, :].bitcast(I32), 0)
            return stacked

        def load_table(a, tag):
            words = reuse.tile([P, T], U32, name="tab_w", tag=tag, align_bytes=64)
            nc.sync.dma_start(words[:].bitcast(I32), tab_words[a].rearrange("p t i -> p (t i)").bitcast(I32))
            return words

        def load_rows(source, name, tag):
            raw = reuse.tile([P, PACK, HALF], F32, name=name, tag=tag, align_bytes=64)
            nc.sync.dma_start(raw[:], source)
            return raw

        def load_wgo(c, tag, row_sets):
            part = reuse.tile([P, PACK, HALF], F32, name="wgo_sb", tag=tag, align_bytes=64)
            for ts in row_sets:
                for q in (0, 2, 1, 3):
                    nc.sync.dma_start(part[32 * q : 32 * q + 32, ts, :], wgo_rows[:, ts, half(c)])
            return part

        def load_x0(g, u, tag):
            pair = reuse.tile([P, 2, S], F32, name="x0_pair", tag=tag, align_bytes=64)
            nc.sync.dma_start(pair[:], x0_rows[g][:, 2 * u : 2 * u + 2, :])
            return [pair[:, 0, :], pair[:, 1, :]]

        def quantize_weight(raw, sign, name, on_vector, tag, bufs):
            dealt = reuse.tile([P, PACK * HALF], BF16, name="dealt", tag=tag, bufs=bufs, align_bytes=64)
            dst = dealt[:].rearrange("p (t m j) -> p m t j", t=PACK, j=PACK)
            src = raw[:].rearrange("p j (m t) -> p m t j", t=PACK)
            if on_vector < P:
                nc.scalar.activation(dst[:, on_vector:, :, :], src[:, on_vector:, :, :], ACT.Copy, scale=sign)
            if on_vector > 0:
                nc.vector.tensor_scalar(dst[:, :on_vector, :, :], src[:, :on_vector, :, :], sign, None, ALU.mult)
            codes = keep.tile([P, HALF], U32, name=name + "_codes", align_bytes=64)
            scales = keep.tile([P, HALF], U8, name=name + "_scales", align_bytes=64)
            nc.vector.quantize_mx(out=codes[:].bitcast(FP8X4), scales=scales[:], in_=dealt[:])
            return codes, scales

        def pick_words(words, a):
            picked = []
            for c in range(HALVES):
                part = keep.tile([P, HALF], U32, name="v_w%d_%d" % (a, c), align_bytes=64)
                entries = pick[:, c * HALF // PER_COL : (c + 1) * HALF // PER_COL]
                nc.vector.tensor_copy(part[:], words[:].indirect(entries))
                picked.append(part)
            return picked

        pick = keep.tile([P, S // PER_COL], U16, name="pick")
        nc.sync.dma_start(pick[:], offs)
        tab_s = load_scale_rows(tab_scales, T, "tab_s")
        w4_s_raw = load_scale_rows(w4_scales, H, "w4_s_raw")
        w4_raw = keep.tile([P, PASSES * 2 * H], U8, name="w4_raw", align_bytes=64)
        nc.sync.dma_start(
            w4_raw[:].bitcast(I32).rearrange("p (a c) -> p a c", a=PASSES),
            w4_words.bitcast(I32).rearrange("a p c -> p a c"),
        )
        tab_w = [load_table(0, "load0")]
        w1_raw = [load_rows(w1_rows[0], "w1_raw", "load2")]
        tab_w.append(load_table(1, "load1"))
        w1_raw.append(load_rows(w1_rows[1], "w1_raw", "load3"))
        place = keep.tile([P, S // PER_COL], U16, name="place")
        nc.sync.dma_start(place[:], offs2)

        v_s = keep.tile([P, S], U8, name="v_s", align_bytes=64)
        nc.vector.tensor_copy(v_s[:], tab_s[:].indirect(pick[:]))
        joined = keep.tile([P, S + H], U8, name="joined", align_bytes=64)
        nc.vector.tensor_copy(
            joined[:, S : S + H].rearrange("p (t m) -> p t m", t=PACK),
            w4_s_raw[:].rearrange("p (m t) -> p t m", t=PACK),
        )
        nc.vector.tensor_copy(joined[:, 0:S].bitcast(I32), v_s[:].bitcast(I32))
        given_s = keep.tile([P, PASSES * (S + H)], U8, name="given_s", align_bytes=64)
        per_quad = 4 * PASSES
        for q in range(QUADS):
            nc.scalar.dma_start(
                given_s[32 * q : 32 * q + 4, :].bitcast(I32).rearrange("r (a t) -> r a t", a=PASSES),
                joined[STACK + per_quad * q : STACK + per_quad * (q + 1), :].bitcast(I32),
            )

        w4_c = keep.tile([P, PASSES * 2 * H], U8, name="w4_c", align_bytes=64)
        nc.vector.tensor_copy(
            w4_c[:].bitcast(U16).rearrange("p (a t m) -> p a t m", a=PASSES, t=PACK),
            w4_raw[:].bitcast(U16).rearrange("p (a m t) -> p a t m", a=PASSES, t=PACK),
        )

        v_w = [pick_words(tab_w[0], 0)]
        tab_w.append(load_table(2, "load0"))
        w1_q = [quantize_weight(w1_raw[0], -1.0, "w1_0", 0, "dealt", 2)]
        w1_raw.append(load_rows(w1_rows[2], "w1_raw", "load2"))
        v_w.append(pick_words(tab_w[1], 1))
        w3_raw = [load_rows(w3_rows[:, :, half(0)], "w3_raw", "load1")]
        w1_q.append(quantize_weight(w1_raw[1], -1.0, "w1_1", 0, "dealt", 2))
        spin_sb = [load_rows(spin_rows[:, :, half(0)], "spin_sb", "load3")]
        v_w.append(pick_words(tab_w[2], 2))
        wgo_sb = [load_wgo(0, "load0", [slice(0, 1), slice(1, PACK)])]
        w1_q.append(quantize_weight(w1_raw[2], -1.0, "w1_2", W1_ON_VECTOR, "dealt", 2))
        spin_sb.append(load_rows(spin_rows[:, :, half(1)], "spin_sb", "load2"))


        def squared_difference(c):
            d_bank = [bank(b) for b in range(PACK)]
            steps = [("w4", 0)]
            for a in range(1, PASSES):
                steps.extend([("w4", a), ("w1", a - 1)])
            steps.append(("w1", PASSES - 1))
            for n, (weight, a) in enumerate(steps):
                base = a * (S + H)
                for b in range(PACK):
                    first = base + c * HALF + b * P
                    for t in range(PACK):
                        if weight == "w1":
                            held = w1_q[a][0][:, t * P : (t + 1) * P].bitcast(FP8X4)
                            held_s = w1_q[a][1][:, t * P : (t + 1) * P]
                        else:
                            held = w4_c[:, 2 * (a * H + t * P) : 2 * (a * H + (t + 1) * P)].bitcast(FP4X4)
                            held_s = given_s[:, base + S + t * P : base + S + (t + 1) * P]
                        nc.tensor.matmul_mx(
                            out=d_bank[b][:, t * P : (t + 1) * P],
                            lhsT=held,
                            lhsT_scale=held_s,
                            rhs=v_w[a][c][:, b * P : (b + 1) * P].bitcast(FP8X4),
                            rhs_scale=given_s[:, first : first + P],
                            start=(n == 0 and t == 0),
                            stop=(n == len(steps) - 1 and t == PACK - 1),
                        )
            sq = reuse.tile([P, PACK, HALF], F32, name="sq", tag="sq%d" % c, align_bytes=64)
            for b in range(PACK):
                nc.scalar.activation(sq[:, b, :], d_bank[b][:], ACT.Square)
            return [sq[:, b, :].rearrange("p (t j) -> p t j", t=PACK) for b in range(PACK)]

        def interleaved(tile, first, width):
            return tile[:, PACK * first : PACK * (first + width)].rearrange("p (c i t) -> p c t i", i=RUN, t=PACK)

        def in_runs(rows4):
            return rows4.rearrange("p t (c i) -> p c t i", i=RUN)

        def h_tiles(c):
            h_bf = reuse.tile([P, PACK * HALF], BF16, name="h_bf", tag="h_bf%d" % c, align_bytes=64)
            h_c = reuse.tile([P, HALF], U32, name="h_c", tag="h_c%d" % c, align_bytes=64)
            h_s = keep.tile([P, HALF], U8, name="h_s%d" % c, align_bytes=64)
            return h_bf, h_c, h_s

        def quantize_columns(codes, scales, values, first, width):
            nc.vector.quantize_mx(
                out=codes[:, first : first + width].bitcast(FP8X4),
                scales=scales[:, first : first + width],
                in_=values[:, PACK * first : PACK * (first + width)],
            )

        def first_half_of_h(sq):
            h_bf, h_c, h_s = h_tiles(0)
            for b in range(PACK):
                nc.vector.tensor_tensor(
                    interleaved(h_bf, b * P, P),
                    in_runs(sq[b]),
                    in_runs(spin_sb[0][:, :, b * P : (b + 1) * P]),
                    ALU.add,
                )
                if (b + 1) * P % QUARTER == 0:
                    quantize_columns(h_c, h_s, h_bf, (b + 1) * P - QUARTER, QUARTER)
            return h_c, h_s

        def second_half_of_h(sq):
            h_bf, h_c, h_s = h_tiles(1)
            for b in range(PACK):
                nc.gpsimd.tensor_tensor(sq[b], sq[b], spin_sb[1][:, :, b * P : (b + 1) * P], ALU.add)
                nc.scalar.copy(interleaved(h_bf, b * P, P), in_runs(sq[b]))
            quantize_columns(h_c, h_s, h_bf, 0, HALF)
            return h_c, h_s

        rows = keep.tile([P, SLICES, S], F32, name="rows")

        def staged(i, first, width):
            if (i, first) == (0, HALF):
                return held_back[:]
            return rows[:, i, first : first + width]

        def weighted_product(i, first, width, k, on_vector):
            g, t = divmod(i, PACK)
            c, inside = divmod(first, HALF)
            acc = bank(k)
            nc.tensor.matmul_mx(
                out=acc[:, 0:width],
                lhsT=w3_q[g][0][:, t * P : (t + 1) * P].bitcast(FP8X4),
                lhsT_scale=w3_q[g][1][:, t * P : (t + 1) * P],
                rhs=h_q[c][0][:, inside : inside + width].bitcast(FP8X4),
                rhs_scale=h_q[c][1][:, inside : inside + width],
                start=True,
                stop=True,
            )
            values = staged(i, first, width)
            factor = wgo_sb[c][:, t, inside : inside + width]
            if on_vector:
                nc.vector.tensor_tensor(values, acc[:, 0:width], factor, ALU.mult)
            else:
                nc.scalar.copy(values, acc[:, 0:width])
                nc.gpsimd.tensor_tensor(values, values, factor, ALU.mult)

        def new_page(i):
            if i == SLICES - 1:
                return reuse.tile([P, PAGE_COLS], F32, name="page", tag="y_bf0", align_bytes=64)
            return reuse.tile([P, PAGE_COLS], F32, name="page", tag="page", bufs=EARLY + 1)

        def scatter(i, first, width):
            entries = place[:, first // PER_COL : (first + width) // PER_COL]
            nc.vector.tensor_copy(pages[i][:].indirect(entries), staged(i, first, width))

        def finish(i):
            g, t = divmod(i, PACK)
            page = pages[i][:, 0:S]
            if i == 0:
                gate = reuse.tile([P, S], F32, name="gate", tag="h_c1", align_bytes=64)
            else:
                gate = reuse.tile([P, S], F32, name="gate", tag="gate", bufs=2)
            dev = reuse.tile([P, S], F32, name="dev", tag="dev", bufs=2)
            y = rows[:, i, :]
            if i < SLICES - 1:
                nc.scalar.activation(gate[:], page, ACT.Sigmoid)
                nc.gpsimd.tensor_tensor(dev[:], page, x0_sb[i], ALU.subtract)
                nc.gpsimd.tensor_tensor(y, dev[:], gate[:], ALU.mult)
                nc.sync.dma_start(y_rows[g][:, t, :], y)
                return
            for c in range(HALVES):
                nc.scalar.activation(gate[:, half(c)], page[:, half(c)], ACT.Sigmoid)
                nc.vector.tensor_tensor(dev[:, half(c)], page[:, half(c)], x0_sb[i][:, half(c)], ALU.subtract)
            for c in range(HALVES):
                nc.vector.tensor_tensor(y[:, half(c)], dev[:, half(c)], gate[:, half(c)], ALU.mult)
                nc.sync.dma_start(y_rows[g][:, t, half(c)], y[:, half(c)])

        def round_rows(g, ts, first, width, copy):
            src = in_runs(rows[:, PACK * g : PACK * (g + 1), first : first + width])
            copy(interleaved(y_bf[g], first, width)[:, :, ts, :], src[:, :, ts, :])

        def planes(g):
            y_c = keep.tile([P, S], U32, name="y_c%d" % g, align_bytes=64)
            y_s = keep.tile([P, S], U8, name="y_s%d" % g, align_bytes=64)
            words_out = out_1[g].rearrange("p m t -> p (m t)").bitcast(I32)
            for c in reversed(range(HALVES)):
                quantize_columns(y_c, y_s, y_bf[g], c * HALF, HALF)
                nc.sync.dma_start(words_out[:, half(c)], y_c[:, half(c)].bitcast(I32))
            for q in range(QUADS):
                queue = nc.scalar if g == GROUPS - 1 and q % 2 == 1 else nc.sync
                queue.dma_start(out_2[g, 4 * q : 4 * q + 4, :].bitcast(I32), y_s[32 * q : 32 * q + 4, :].bitcast(I32))

        pages = [new_page(i) for i in range(EARLY)]
        w3_q = [quantize_weight(w3_raw[0], 1.0, "w3_0", P, "dealt", 2)]
        w3_raw.append(load_rows(w3_rows[:, :, half(1)], "w3_raw", "load1"))
        h_q = [first_half_of_h(squared_difference(0))]
        wgo_sb.append(load_wgo(1, "load3", [slice(0, PACK)]))

        opening = [(0, 0, QUARTER), (0, QUARTER, QUARTER)] + [(i, 0, HALF) for i in range(1, EARLY)]
        for n, (i, first, width) in enumerate(opening):
            weighted_product(i, first, width, PACK + n % PACK, i == 0)
            scatter(i, first, width)

        h_q.append(second_half_of_h(squared_difference(1)))
        w3_q.append(quantize_weight(w3_raw[1], 1.0, "w3_1", 0, "sq1", 1))
        held_back = reuse.tile([P, HALF], F32, name="held_back", tag="sq1", align_bytes=64)
        later = [(i, 1) for i in range(EARLY)] + [(i, c) for i in range(EARLY, SLICES) for c in range(HALVES)]
        for n, (i, c) in enumerate(later):
            on_vector = i == 0 or i >= SLICES - ON_VECTOR
            weighted_product(i, c * HALF, HALF, n % (2 * PACK), on_vector)
        x0_sb = load_x0(0, 0, "load1") + load_x0(0, 1, "load2") + load_x0(1, 0, "load0") + load_x0(1, 1, "load3")
        for i in range(EARLY):
            scatter(i, HALF, HALF)

        y_bf = [
            reuse.tile([P, PACK * S], BF16, name="y_bf", tag="y_bf%d" % g, align_bytes=64) for g in range(GROUPS)
        ]
        for i in range(SLICES):
            following = i + 1
            if following == SLICES - 1:
                planes(0)
            if EARLY <= following < SLICES:
                pages.append(new_page(following))
                scatter(following, 0, S)
            finish(i)
            if i == PACK:
                for first in range(0, S, QUARTER):
                    round_rows(0, slice(0, PACK), first, QUARTER, nc.scalar.copy)
            if i == SLICES - 2:
                for c in range(HALVES):
                    round_rows(1, slice(0, 2), c * HALF, HALF, nc.scalar.copy)
        round_rows(1, slice(2, PACK), 0, HALF, nc.scalar.copy)
        round_rows(1, slice(2, PACK), HALF, HALF, nc.vector.tensor_copy)
        planes(1)
